import numpy as np
import ml_dtypes


def mxq(x, axis, fmt="e4m3"):
    dtype, down = {"e4m3": (ml_dtypes.float8_e4m3fn, 7), "e5m2": (ml_dtypes.float8_e5m2, 14)}[fmt]
    v = np.moveaxis(np.asarray(x, np.float32).astype(ml_dtypes.bfloat16).astype(np.float64), axis, -1)
    blocks = v.reshape(v.shape[:-1] + (-1, 32))
    amax = np.abs(blocks).max(-1, keepdims=True)
    byte = np.maximum(np.where(amax > 0, np.frexp(amax)[1] - 1 + 127, 0) - down, 1)
    scale = np.exp2(byte - 127.0)
    codes = (blocks / scale).astype(np.float32).astype(dtype).astype(np.float64)
    return np.moveaxis((codes * scale).reshape(v.shape), -1, axis)


WIDE = False


def mx_kscale(k):
    if not WIDE:
        return np.ones(k)
    levels = np.array([30, -30])
    if k % 512:
        return np.exp2(np.random.permutation(np.resize(levels, k // 32))).repeat(32)
    a = np.empty((k // 512, 16))
    for p in range(k // 512):
        a[p, :8] = np.random.permutation(np.resize(levels, 8))
        for g in range(8):
            far = levels[np.abs(levels - a[p, g]) >= 10]
            a[p, g + 8] = far[np.random.randint(len(far))]
    return np.exp2(a.ravel()).repeat(32)


BF16 = ml_dtypes.bfloat16


def bf(x):
    return np.asarray(x, np.float32).astype(BF16)


def f64(x):
    return np.asarray(x).astype(np.float64)


E2M1 = np.array([0.0, 0.5, 1.0, 1.5, 2.0, 3.0, 4.0, 6.0, -0.0, -0.5, -1.0, -1.5, -2.0, -3.0, -4.0, -6.0])


def pack_weight(w, fmt):
    k, n = w.shape
    w = f64(bf(w)).reshape(k // 32, 32, n)
    amax = np.abs(w).max(1)
    if fmt == "e4m3":
        byte = np.frexp(amax)[1] - 1 + 127 - 7
    else:
        mant, ex = np.frexp(amax / 6.0)
        byte = np.where(mant > 0.5, ex, ex - 1) + 127
    byte = np.clip(np.where(amax > 0, byte, 1), 1, 254)
    scaled = (w * np.exp2(127.0 - byte)[:, None, :]).reshape(k, n).astype(np.float32)
    by_word = np.ascontiguousarray(scaled.reshape(k // 512, 128, 4, n).transpose(0, 1, 3, 2))
    if fmt == "e4m3":
        words = by_word.astype(ml_dtypes.float8_e4m3fn).view(np.uint8)
    else:
        c = by_word.astype(ml_dtypes.float4_e2m1fn).view(np.uint8) & 0xF
        words = c[..., 0::2] | (c[..., 1::2] << 4)
    return np.ascontiguousarray(words), np.ascontiguousarray(byte.astype(np.uint8).reshape(k // 512, 16, n))


def unpack_weight(words, scales, fmt):
    g, p, n, _ = words.shape
    if fmt == "e4m3":
        vals = np.ascontiguousarray(words).view(ml_dtypes.float8_e4m3fn).astype(np.float64)
    else:
        nib = np.empty((g, p, n, 4), np.uint8)
        nib[..., 0::2] = words & 0xF
        nib[..., 1::2] = words >> 4
        vals = E2M1[nib]
    vals = vals * np.repeat(np.exp2(scales.astype(np.float64) - 127.0), 8, axis=1)[..., None]
    return vals.transpose(0, 1, 3, 2).reshape(g * 512, n)
def pack4(w):
    words, scales = pack_weight(w, "e2m1")
    return words.reshape(words.shape[0], 128, -1), scales


def unpack4(words, scales):
    return unpack_weight(words.reshape(words.shape[0], 128, -1, 2), scales, "e2m1")


M, KC, KR, F, N = 1024, 2048, 512, 1536, 512


def setup_inputs():
    s = mx_kscale(KC)
    u = mx_kscale(KR)
    t = mx_kscale(F)
    wc = np.random.standard_normal((KC, F)) / np.sqrt(KC) / s[:, None] * t
    wc_words, wc_scales = pack4(wc)
    return {"cam": bf(np.random.standard_normal((M, KC)) * s),
            "wc_words": wc_words,
            "wc_scales": wc_scales,
            "b": bf(0.4 * np.random.standard_normal(F) * t),
            "radar": bf(1.5 * np.random.standard_normal((M, KR)) * u),
            "wr": bf(np.random.standard_normal((KR, F)) / np.sqrt(KR) / u[:, None]),
            "wo": bf(np.random.standard_normal((F, N)) / np.sqrt(F) / t[:, None])}


def reference(cam, wc_words, wc_scales, b, radar, wr, wo):
    wc = unpack4(wc_words, wc_scales)
    v = mxq(f64(cam), 1, "e4m3") @ wc
    z = mxq(f64(radar), 1, "e4m3") @ mxq(f64(wr), 0, "e4m3")
    h = (v + f64(b)) * (1.0 / (1.0 + np.exp(-z)))
    return mxq(h, 1, "e5m2") @ mxq(f64(wo), 0, "e4m3")

@@ -1,0 +1,397 @@
+from contextlib import ExitStack
+
+import concourse.mybir as mybir
+from concourse.masks import make_identity
+
+M, KC, KR, F, N = 1024, 2048, 512, 1536, 512
+FLOPS = 2 * M * (KC * F + KR * F + F * N)
+
+F32 = mybir.dt.float32
+BF16 = mybir.dt.bfloat16
+I32 = mybir.dt.int32
+U32 = mybir.dt.uint32
+U8 = mybir.dt.uint8
+E4M3 = mybir.dt.float8_e4m3fn_x4
+E5M2 = mybir.dt.float8_e5m2_x4
+E2M1 = mybir.dt.float4_e2m1fn_x4
+SIGMOID = mybir.ActivationFunctionType.Sigmoid
+ADD = mybir.AluOpType.add
+MULT = mybir.AluOpType.mult
+
+P = 128
+PACK = 4
+W = 512
+HALVES = M // W
+CAM_PASSES = KC // W
+RADAR = CAM_PASSES
+GROUPS = F // W
+TILES = W // P
+UNITS = [(0, 0), (1, 0), (0, 1), (0, 2), (1, 1), (1, 2)]
+
+
+def tile_camera_radar_gated_fusion_s9_kernel(tc, cam, wc_words, wc_scales, b, radar, wr, wo, out):
+    nc = tc.nc
+    with ExitStack() as ctx:
+        sb = ctx.enter_context(tc.tile_pool(name="sb", bufs=1))
+        ps = ctx.enter_context(tc.psum_pool(name="ps", bufs=1))
+        ctx.enter_context(tc.manual_schedule())
+
+        def tiles(name, count, shape, dtype):
+            return [sb.tile(shape, dtype, name="%s%d" % (name, i), align_bytes=64) for i in range(count)]
+
+        def quantised(name, count):
+            return list(zip(tiles(name + "_codes", count, [P, W], U32), tiles(name + "_scales", count, [P, W], U8)))
+
+        banks = [ps.tile([P, W], F32, name="bank%d" % i) for i in range(8)]
+        ident = sb.tile([P, P], F32, name="ident")
+        warm = sb.tile([P, 8], F32, name="warm")
+        b_rows = sb.tile([P, P], BF16, name="b_rows")
+        b_rows32 = sb.tile([P, P], F32, name="b_rows32")
+        bias = sb.tile([P, 16], F32, name="bias")
+        chunks = CAM_PASSES + 1
+        act_raw = tiles("act_raw", HALVES * chunks, [P, TILES, W], BF16)
+        act_q = quantised("act", HALVES * chunks)
+        act_stage = tiles("act_stage", 3, [P, PACK * W], BF16)
+        wc_raw = tiles("wc_raw", GROUPS, [P, CAM_PASSES, 256], I32)
+        wc_codes = tiles("wc_codes", GROUPS, [P, PACK, CAM_PASSES, 256], U8)
+        sc_first = sb.tile([P, CAM_PASSES, 128], I32, name="sc_first")
+        sc_rest = sb.tile([P, CAM_PASSES, 256], I32, name="sc_rest")
+        wc_sc = tiles("wc_sc", GROUPS, [P, PACK, CAM_PASSES, P], U8)
+        wr_raw = tiles("wr_raw", GROUPS, [P, PACK, W], BF16)
+        wo_raw = tiles("wo_raw", GROUPS, [P, PACK, W], BF16)
+        w_stage = tiles("w_stage", 2, [P, PACK * W], BF16)
+        wr_q = quantised("wr", GROUPS)
+        wo_q = quantised("wo", GROUPS)
+        gate = tiles("gate", 4, [P, W], F32)
+        h_raw = tiles("h_raw", 2, [P, PACK, W], BF16)
+        h_stage = tiles("h_stage", 2, [P, PACK * W], BF16)
+        h_q = quantised("h", HALVES * GROUPS)
+        result = tiles("result", HALVES * TILES, [P, W], F32)
+
+        def load_act(h, c, lo=0, hi=TILES):
+            src = radar if c == RADAR else cam[:, c * W:(c + 1) * W]
+            rows = src[h * W:(h + 1) * W, :].rearrange("(i p) k -> p i k", p=P)
+            nc.sync.dma_start(out=act_raw[h * chunks + c][:, lo:hi, :], in_=rows[:, lo:hi, :])
+
+        def load_wc(G, lo=0, hi=CAM_PASSES):
+            src = wc_words.bitcast(I32)[lo:hi, :, 256 * G:256 * (G + 1)]
+            nc.sync.dma_start(out=wc_raw[G][:, lo:hi, :], in_=src.rearrange("g p w -> p g w"))
+
+        def load_scales(queue, dst, lo, hi):
+            for Q in range(4):
+                src = wc_scales.bitcast(I32)[:, 4 * Q:4 * Q + 4, lo:hi]
+                queue.dma_start(out=dst[32 * Q:32 * Q + 4, :, :], in_=src.rearrange("g r w -> r g w"))
+
+        def load_wr(G):
+            src = wr[:, G * W:(G + 1) * W].rearrange("(p j) c -> p j c", j=PACK)
+            nc.sync.dma_start(out=wr_raw[G][:], in_=src)
+
+        def load_wo(G):
+            src = wo[G * W:(G + 1) * W, :].rearrange("(r t e) n -> e r t n", t=4, e=4)
+            for e in range(4):
+                nc.sync.dma_start(out=wo_raw[G][e:P:4, :, :], in_=src[e])
+
+        def load_bias():
+            src = b.rearrange("(G r t e) -> G t r e", G=GROUPS, t=4, e=4)
+            for G in range(GROUPS):
+                nc.sync.dma_start(out=b_rows[4 * G:4 * G + 4, :].rearrange("t (r e) -> t r e", e=4), in_=src[G])
+
+        def turn(h, c):
+            words = act_raw[h * chunks + c][:].bitcast(F32)
+            pair = [banks.pop(0), banks.pop(0)]
+            for i in range(TILES):
+                for u in range(2):
+                    col = (2 * (i % 2) + u) * P
+                    nc.tensor.transpose(pair[i // 2][:, col:col + P], words[:, i, u:256:2], ident[:])
+            return pair
+
+        def copy_on(engine, out, in_):
+            if engine is nc.scalar:
+                nc.scalar.copy(out=out, in_=in_)
+            else:
+                nc.vector.tensor_copy(out=out, in_=in_)
+
+        def unload(h, c, pair, j, engine):
+            stage = act_stage[(h * chunks + c) % 3][:].bitcast(F32)
+            copy_on(engine, stage[:, j * W:(j + 1) * W].rearrange("p (i r u) -> p i r u", i=2, u=2),
+                    pair[j][:].rearrange("p (i u r) -> p i r u", i=2, u=2))
+            banks.append(pair[j])
+
+        def quantise(dst, src, fmt, lo=0, hi=W):
+            nc.vector.quantize_mx(out=dst[0][:, lo:hi].bitcast(fmt), scales=dst[1][:, lo:hi], in_=src[:, PACK * lo:PACK * hi])
+
+        def quantise_act(h, c):
+            quantise(act_q[h * chunks + c], act_stage[(h * chunks + c) % 3], E4M3)
+
+        def order_wc(G, lo=0, hi=CAM_PASSES):
+            dst = wc_codes[G][:].bitcast(I32)[:, :, lo:hi, :].rearrange("p t g (r e) -> p t g r e", e=2)
+            src = wc_raw[G][:, lo:hi, :].rearrange("p g (r t e) -> p t g r e", t=4, e=2)
+            nc.vector.tensor_copy(out=dst, in_=src)
+
+        def order_scales(G):
+            raw = sc_first[:] if G == 0 else sc_rest[:, :, 128 * (G - 1):128 * G]
+            nc.vector.tensor_copy(out=wc_sc[G][:].bitcast(I32), in_=raw.rearrange("p g (r t) -> p t g r", t=4))
+
+        def weave_wr(G, t, engine):
+            dst = w_stage[G % 2][:, t * W:(t + 1) * W].rearrange("p (r e j) -> p r j e", e=4, j=4)
+            src = wr_raw[G][:].rearrange("p j (r t e) -> p t r j e", t=4, e=4)[:, t]
+            copy_on(engine, dst, src)
+
+        def weave(dst, src, engine, lo=0, hi=W):
+            copy_on(engine, dst[:, PACK * lo:PACK * hi].rearrange("p (c i t) -> p c t i", i=4, t=PACK),
+                    src[:, :, lo:hi].rearrange("p t (c i) -> p c t i", i=4))
+
+        def cam_pass(bank, h, G, t, g):
+            codes, scales = act_q[h * chunks + g]
+            nc.tensor.matmul_mx(out=bank[:], lhsT=wc_codes[G][:, t, g, :].bitcast(E2M1), lhsT_scale=wc_sc[G][:, t, g, :],
+                                rhs=codes[:].bitcast(E4M3), rhs_scale=scales[:], start=(g == 0), stop=(g == CAM_PASSES - 1))
+
+        def gate_of(h, G, t):
+            bank = banks.pop(0)
+            codes, scales = act_q[h * chunks + RADAR]
+            cols = slice(t * P, (t + 1) * P)
+            nc.tensor.matmul_mx(out=bank[:], lhsT=wr_q[G][0][:, cols].bitcast(E4M3), lhsT_scale=wr_q[G][1][:, cols],
+                                rhs=codes[:].bitcast(E4M3), rhs_scale=scales[:], start=True, stop=True)
+            nc.scalar.activation(out=gate[t][:], in_=bank[:], func=SIGMOID)
+            banks.append(bank)
+
+        def fuse(bank, h, G, t, lo=0, hi=W):
+            nc.vector.scalar_tensor_tensor(out=h_raw[UNITS.index((h, G)) % 2][:, t, lo:hi], in0=bank[:, lo:hi], scalar=bias[:, 4 * G + t:4 * G + t + 1],
+                                           in1=gate[t][:, lo:hi], op0=ADD, op1=MULT)
+            if hi == W:
+                banks.append(bank)
+
+        def cam_group(h, G, t):
+            bank = banks.pop(0)
+            for g in range(CAM_PASSES):
+                cam_pass(bank, h, G, t, g)
+            return bank
+
+        def cam_round(acc, h, g):
+            for t in range(PACK):
+                cam_pass(acc[t], h, 0, t, g)
+
+        def head_pass(bank, h, i, G):
+            codes, scales = h_q[h * GROUPS + G]
+            cols = slice(i * P, (i + 1) * P)
+            nc.tensor.matmul_mx(out=bank[:], lhsT=codes[:, cols].bitcast(E5M2), lhsT_scale=scales[:, cols],
+                                rhs=wo_q[G][0][:].bitcast(E4M3), rhs_scale=wo_q[G][1][:],
+                                start=(G == 0), stop=(G == GROUPS - 1))
+
+        def store(bank, h, i, engine):
+            copy_on(engine, result[h * TILES + i][:], bank[:])
+            banks.append(bank)
+            row = h * W + i * P
+            nc.sync.dma_start(out=out[row:row + P, :], in_=result[h * TILES + i][:])
+
+        S, V = nc.scalar, nc.vector
+
+        def weave_h(n, engine=V, lo=0, hi=W):
+            weave(h_stage[n % 2], h_raw[n % 2], engine, lo, hi)
+
+        def quantise_h(n, lo=0, hi=W):
+            h, G = UNITS[n]
+            quantise(h_q[h * GROUPS + G], h_stage[n % 2], E5M2, lo, hi)
+
+        def head_tile(h, i):
+            bank = banks.pop(0)
+            for G in range(GROUPS):
+                head_pass(bank, h, i, G)
+            store(bank, h, i, S)
+
+        def weave_wo(G, engine, lo=0, hi=W):
+            weave(w_stage[(G + 1) % 2], wo_raw[G], engine, lo, hi)
+
+        def quantise_wo(G):
+            quantise(wo_q[G], w_stage[(G + 1) % 2], E4M3)
+
+        def quantise_wr(G):
+            quantise(wr_q[G], w_stage[G % 2], E4M3)
+
+        load_act(0, 0, 0, 2)
+        load_act(0, 0, 2, 4)
+        load_act(0, 1)
+        nc.vector.memset(sc_first[:], 0)
+        nc.vector.memset(warm[:, 0:1], 0.0)
+        nc.vector.memset(b_rows[:], 0.0)
+        nc.vector.memset(sc_rest[:], 0)
+        make_identity(nc, ident[:])
+        nc.scalar.activation(out=warm[:, 1:2], in_=warm[:, 0:1], func=SIGMOID)
+        load_scales(nc.sync, sc_first, 0, 128)
+        load_wc(0, 0, 2)
+        load_act(0, 2)
+        load_wc(0, 2, 4)
+        load_act(0, RADAR)
+        load_bias()
+        load_wr(0)
+        load_act(0, 3)
+        load_act(1, 0)
+        load_act(1, 1)
+        load_wc(1)
+        load_scales(nc.sync, sc_rest, 128, 384)
+        load_act(1, 2)
+        load_wr(1)
+        load_act(1, RADAR)
+        load_wc(2)
+        load_act(1, 3)
+        load_wr(2)
+        for G in range(GROUPS):
+            load_wo(G)
+
+        acc = [banks.pop() for t in range(PACK)]
+        pair = turn(0, 0)
+        unload(0, 0, pair, 0, S)
+        unload(0, 0, pair, 1, V)
+        pair = turn(0, 1)
+        order_scales(0)
+        quantise_act(0, 0)
+        order_wc(0, 0, 2)
+        unload(0, 1, pair, 0, S)
+        unload(0, 1, pair, 1, S)
+        cam_round(acc, 0, 0)
+        quantise_act(0, 1)
+        pair = turn(0, 2)
+        unload(0, 2, pair, 0, S)
+        order_wc(0, 2, 4)
+        unload(0, 2, pair, 1, V)
+        nc.vector.tensor_copy(out=b_rows32[:], in_=b_rows[:])
+        quantise_act(0, 2)
+        cam_round(acc, 0, 1)
+        pair = turn(0, RADAR)
+        bank = banks.pop(0)
+        nc.tensor.transpose(bank[:, 0:P], b_rows32[:], ident[:])
+        unload(0, RADAR, pair, 0, S)
+        unload(0, RADAR, pair, 1, S)
+        nc.scalar.copy(out=bias[:], in_=bank[:, 0:16])
+        banks.append(bank)
+        cam_round(acc, 0, 2)
+        for t in range(PACK):
+            weave_wr(0, t, V)
+        quantise_act(0, RADAR)
+        quantise_wr(0)
+        pair = turn(0, 3)
+        unload(0, 3, pair, 0, S)
+        unload(0, 3, pair, 1, V)
+        gate_of(0, 0, 0)
+        gate_of(0, 0, 1)
+        pair = turn(1, 0)
+        quantise_act(0, 3)
+        unload(1, 0, pair, 0, S)
+        unload(1, 0, pair, 1, V)
+        gate_of(0, 0, 2)
+        gate_of(0, 0, 3)
+        cam_round(acc, 0, 3)
+        quantise_act(1, 0)
+
+        pair = turn(1, 1)
+        unload(1, 1, pair, 0, S)
+        unload(1, 1, pair, 1, S)
+        spare = list(banks)
+        for t in range(PACK):
+            fuse(acc[t], 0, 0, t)
+        banks.clear()
+        banks.extend(spare)
+        quantise_act(1, 1)
+        cam_round(acc, 1, 0)
+        pair = turn(1, 2)
+        unload(1, 2, pair, 0, S)
+        unload(1, 2, pair, 1, S)
+        weave_h(0)
+        order_wc(1)
+        quantise_act(1, 2)
+        weave_wr(1, 0, S)
+        weave_wr(1, 1, S)
+        cam_round(acc, 1, 1)
+        pair = turn(1, RADAR)
+        unload(1, RADAR, pair, 0, S)
+        unload(1, RADAR, pair, 1, S)
+        quantise_h(0)
+        order_scales(1)
+        weave_wr(1, 3, V)
+        quantise_act(1, RADAR)
+        weave_wr(1, 2, S)
+        cam_round(acc, 1, 2)
+        pair = turn(1, 3)
+        unload(1, 3, pair, 0, S)
+        order_wc(2)
+        unload(1, 3, pair, 1, V)
+        quantise_wr(1)
+        quantise_act(1, 3)
+        order_scales(2)
+        gate_of(1, 0, 0)
+        gate_of(1, 0, 1)
+        ahead = cam_group(0, 1, 0)
+        gate_of(1, 0, 2)
+        weave_wr(2, 0, V)
+        weave_wr(2, 1, V)
+        cam_pass(acc[0], 1, 0, 0, 3)
+        cam_pass(acc[1], 1, 0, 1, 3)
+        gate_of(1, 0, 3)
+        cam_pass(acc[2], 1, 0, 2, 3)
+        cam_pass(acc[3], 1, 0, 3, 3)
+        for t in range(PACK):
+            fuse(acc[t], 1, 0, t)
+
+        side = {
+            (2, 0): [lambda: weave_wr(2, 2, S), lambda: weave_wr(2, 3, S)],
+            (2, 1): [lambda: quantise_wr(2), lambda: weave_wo(0, S, 0, 128)],
+            (2, 2): [lambda: weave_wo(0, S, 128, 256)],
+            (2, 3): [lambda: weave_wo(0, S, 256, 384), lambda: weave_wo(0, V, 384, 512)],
+            (3, 0): [lambda: weave_wo(1, S, 0, 128), lambda: quantise_wo(0)],
+            (3, 1): [lambda: weave_wo(1, S, 128, 256)],
+            (3, 2): [lambda: weave_wo(1, S, 256, 384), lambda: weave_wo(1, V, 384, 512)],
+            (3, 3): [lambda: weave_wo(2, S, 0, 128), lambda: quantise_wo(1)],
+            (4, 0): [lambda: weave_wo(2, S, 128, 256)],
+            (4, 1): [lambda: weave_wo(2, S, 256, 384), lambda: weave_wo(2, V, 384, 512)],
+            (4, 2): [lambda: quantise_wo(2)],
+            (5, 0): [lambda: head_tile(0, 0)],
+            (5, 1): [lambda: head_tile(0, 1)],
+            (5, 2): [lambda: head_tile(0, 2)],
+        }
+        last = len(UNITS) - 1
+        for n in range(2, last + 1):
+            h, G = UNITS[n]
+            for t in range(PACK):
+                if n == 2:
+                    bank = ahead if t == 0 else cam_group(h, G, t)
+                    gate_of(h, G, t)
+                else:
+                    gate_of(h, G, t)
+                    bank = cam_group(h, G, t)
+                for job in side.get((n, t), []):
+                    job()
+                if (n, t) == (last, PACK - 1):
+                    break
+                fuse(bank, h, G, t)
+                if t == 0:
+                    weave_h(n - 1)
+                if t == 1:
+                    quantise_h(n - 1)
+
+        early = banks.pop(0)
+        for g in range(GROUPS):
+            head_pass(early, 0, 3, g)
+        acc = [banks.pop(0) for i in range(TILES)]
+        fuse(bank, h, G, t, 0, P)
+        fuse(bank, h, G, t, P, 2 * P)
+        weave_h(last, V, 0, P)
+        weave_h(last, S, P, 2 * P)
+        fuse(bank, h, G, t, 2 * P, 4 * P)
+        quantise_h(last, 0, P)
+        weave_h(last, V, 2 * P, 3 * P)
+        quantise_h(last, P, 2 * P)
+        store(early, 0, 3, S)
+        weave_h(last, V, 3 * P, 4 * P)
+        quantise_h(last, 2 * P, 3 * P)
+        for G in range(GROUPS - 1):
+            head_pass(acc[0], 1, 0, G)
+        for G in range(GROUPS - 1):
+            head_pass(acc[1], 1, 1, G)
+        head_pass(acc[0], 1, 0, 2)
+        head_pass(acc[1], 1, 1, 2)
+        quantise_h(last, 3 * P, 4 * P)
+        for i in (2, 3):
+            for G in range(GROUPS):
+                head_pass(acc[i], 1, i, G)
+        for i in range(TILES):
+            store(acc[i], 1, i, S if i % 2 == 0 else V)

@@ -26,6 +26,8 @@ CAM_PASSES = KC // W
 RADAR = CAM_PASSES
 GROUPS = F // W
 TILES = W // P
+ORDER = [(0, 0), (0, 1), (0, 2), (0, 3), (0, RADAR), (1, 0), (1, 1), (1, 2), (1, RADAR), (1, 3)]
+SPLIT = [(0, 1, 0), (0, 2, 0), (0, 3, 0), (0, 3, 1), (0, 2, 1), (0, 4, 0), (0, 4, 1), (1, 1, 0), (1, 1, 1), (1, 2, 0), (1, 3, 0), (1, 2, 1), (1, 3, 1)]
 UNITS = [(0, 0), (1, 0), (0, 1), (0, 2), (1, 1), (1, 2)]
 
 
@@ -39,8 +41,12 @@ def tile_camera_radar_gated_fusion_s9_kernel(tc, cam, wc_words, wc_scales, b, ra
         def tiles(name, count, shape, dtype):
             return [sb.tile(shape, dtype, name="%s%d" % (name, i), align_bytes=64) for i in range(count)]
 
+        def stack(name, count, shape, dtype):
+            whole = sb.tile([P, count] + shape[1:], dtype, name=name, align_bytes=256)
+            return [whole[:, i] for i in range(count)]
+
         def quantised(name, count):
-            return list(zip(tiles(name + "_codes", count, [P, W], U32), tiles(name + "_scales", count, [P, W], U8)))
+            return list(zip(stack(name + "_codes", count, [P, W], U32), stack(name + "_scales", count, [P, W], U8)))
 
         banks = [ps.tile([P, W], F32, name="bank%d" % i) for i in range(8)]
         ident = sb.tile([P, P], F32, name="ident")
@@ -49,29 +55,36 @@ def tile_camera_radar_gated_fusion_s9_kernel(tc, cam, wc_words, wc_scales, b, ra
         b_rows32 = sb.tile([P, P], F32, name="b_rows32")
         bias = sb.tile([P, 16], F32, name="bias")
         chunks = CAM_PASSES + 1
-        act_raw = tiles("act_raw", HALVES * chunks, [P, TILES, W], BF16)
+        cam_raw = tiles("cam_raw", HALVES * 2, [P, TILES, 2 * W], BF16)
+        radar_raw = tiles("radar_raw", HALVES, [P, TILES, W], BF16)
+        reused = [cam_raw[i // 2][:].rearrange("p i k -> p (i k)")[:, (i % 2) * PACK * W:(i % 2 + 1) * PACK * W] for i in range(8)]
+        act_split = tiles("act_split", 6, [P, 2, 2, P], F32)
         act_q = quantised("act", HALVES * chunks)
         act_stage = tiles("act_stage", 3, [P, PACK * W], BF16)
         wc_raw = tiles("wc_raw", GROUPS, [P, CAM_PASSES, 256], I32)
-        wc_codes = tiles("wc_codes", GROUPS, [P, PACK, CAM_PASSES, 256], U8)
+        wc_codes = stack("wc_codes", GROUPS, [P, PACK, CAM_PASSES, 256], U8)
         sc_first = sb.tile([P, CAM_PASSES, 128], I32, name="sc_first")
         sc_rest = sb.tile([P, CAM_PASSES, 256], I32, name="sc_rest")
-        wc_sc = tiles("wc_sc", GROUPS, [P, PACK, CAM_PASSES, P], U8)
+        wc_sc = stack("wc_sc", GROUPS, [P, PACK, CAM_PASSES, P], U8)
         wr_raw = tiles("wr_raw", GROUPS, [P, PACK, W], BF16)
         wo_raw = tiles("wo_raw", GROUPS, [P, PACK, W], BF16)
         w_stage = tiles("w_stage", 2, [P, PACK * W], BF16)
         wr_q = quantised("wr", GROUPS)
         wo_q = quantised("wo", GROUPS)
-        gate = tiles("gate", 4, [P, W], F32)
-        h_raw = tiles("h_raw", 2, [P, PACK, W], BF16)
-        h_stage = tiles("h_stage", 2, [P, PACK * W], BF16)
+        gate = tiles("gate", 6, [P, W], F32)
+        h_raw = [reused[n].rearrange("p (t m) -> p t m", t=PACK) for n in range(6)]
+        h_own = tiles("h_stage", 2, [P, PACK * W], BF16)
+        h_stage = [h_own[0], act_stage[1], h_own[1], act_stage[2], act_stage[0], h_own[0]]
+        wo_stage = [radar_raw[0][:].rearrange("p i k -> p (i k)"), reused[6], reused[7]]
         h_q = quantised("h", HALVES * GROUPS)
         result = tiles("result", HALVES * TILES, [P, W], F32)
 
-        def load_act(h, c, lo=0, hi=TILES):
-            src = radar if c == RADAR else cam[:, c * W:(c + 1) * W]
-            rows = src[h * W:(h + 1) * W, :].rearrange("(i p) k -> p i k", p=P)
-            nc.sync.dma_start(out=act_raw[h * chunks + c][:, lo:hi, :], in_=rows[:, lo:hi, :])
+        def load_cam(h, d, lo, hi):
+            rows = cam[h * W:(h + 1) * W, 2 * W * d:2 * W * (d + 1)].rearrange("(p i) k -> p i k", i=TILES)
+            nc.sync.dma_start(out=cam_raw[2 * h + d][:, lo:hi, :], in_=rows[:, lo:hi, :])
+
+        def load_radar(h):
+            nc.sync.dma_start(out=radar_raw[h][:], in_=radar[h * W:(h + 1) * W, :].rearrange("(p i) k -> p i k", i=TILES))
 
         def load_wc(G, lo=0, hi=CAM_PASSES):
             src = wc_words.bitcast(I32)[lo:hi, :, 256 * G:256 * (G + 1)]
@@ -96,14 +109,15 @@ def tile_camera_radar_gated_fusion_s9_kernel(tc, cam, wc_words, wc_scales, b, ra
             for G in range(GROUPS):
                 nc.sync.dma_start(out=b_rows[4 * G:4 * G + 4, :].rearrange("t (r e) -> t r e", e=4), in_=src[G])
 
-        def turn(h, c):
-            words = act_raw[h * chunks + c][:].bitcast(F32)
-            pair = [banks.pop(0), banks.pop(0)]
-            for i in range(TILES):
-                for u in range(2):
-                    col = (2 * (i % 2) + u) * P
-                    nc.tensor.transpose(pair[i // 2][:, col:col + P], words[:, i, u:256:2], ident[:])
-            return pair
+        S, V = nc.scalar, nc.vector
+        held = {}
+
+        def take(key):
+            held[key] = banks.pop(0)
+            return held[key]
+
+        def give(key):
+            banks.append(held[key])
 
         def copy_on(engine, out, in_):
             if engine is nc.scalar:
@@ -111,17 +125,32 @@ def tile_camera_radar_gated_fusion_s9_kernel(tc, cam, wc_words, wc_scales, b, ra
             else:
                 nc.vector.tensor_copy(out=out, in_=in_)
 
-        def unload(h, c, pair, j, engine):
-            stage = act_stage[(h * chunks + c) % 3][:].bitcast(F32)
+        def halves(h, c):
+            raw = radar_raw[h][:] if c == RADAR else cam_raw[2 * h + c // 2][:, :, (c % 2) * W:(c % 2 + 1) * W]
+            return raw.bitcast(F32).rearrange("p i (w u) -> p i u w", u=2)
+
+        def split(engine, h, c, j):
+            copy_on(engine, act_split[SPLIT.index((h, c, j)) % 6][:], halves(h, c)[:, 2 * j:2 * j + 2])
+
+        def turn(h, c, j):
+            words = act_split[SPLIT.index((h, c, j)) % 6][:] if (h, c, j) in SPLIT else halves(h, c)[:, 2 * j:2 * j + 2]
+            bank = take(("turn", h, c, j))
+            for i in range(2):
+                for u in range(2):
+                    col = (2 * i + u) * P
+                    nc.tensor.transpose(bank[:, col:col + P], words[:, i, u, :], ident[:])
+
+        def unload(engine, h, c, j):
+            stage = act_stage[ORDER.index((h, c)) % 3][:].bitcast(F32)
             copy_on(engine, stage[:, j * W:(j + 1) * W].rearrange("p (i r u) -> p i r u", i=2, u=2),
-                    pair[j][:].rearrange("p (i u r) -> p i r u", i=2, u=2))
-            banks.append(pair[j])
+                    held[("turn", h, c, j)][:].rearrange("p (i u r) -> p i r u", i=2, u=2))
+            give(("turn", h, c, j))
 
         def quantise(dst, src, fmt, lo=0, hi=W):
             nc.vector.quantize_mx(out=dst[0][:, lo:hi].bitcast(fmt), scales=dst[1][:, lo:hi], in_=src[:, PACK * lo:PACK * hi])
 
-        def quantise_act(h, c):
-            quantise(act_q[h * chunks + c], act_stage[(h * chunks + c) % 3], E4M3)
+        def quantise_act(h, c, lo=0, hi=W):
+            quantise(act_q[h * chunks + c], act_stage[ORDER.index((h, c)) % 3], E4M3, lo, hi)
 
         def order_wc(G, lo=0, hi=CAM_PASSES):
             dst = wc_codes[G][:].bitcast(I32)[:, :, lo:hi, :].rearrange("p t g (r e) -> p t g r e", e=2)
@@ -132,266 +161,375 @@ def tile_camera_radar_gated_fusion_s9_kernel(tc, cam, wc_words, wc_scales, b, ra
             raw = sc_first[:] if G == 0 else sc_rest[:, :, 128 * (G - 1):128 * G]
             nc.vector.tensor_copy(out=wc_sc[G][:].bitcast(I32), in_=raw.rearrange("p g (r t) -> p t g r", t=4))
 
-        def weave_wr(G, t, engine):
-            dst = w_stage[G % 2][:, t * W:(t + 1) * W].rearrange("p (r e j) -> p r j e", e=4, j=4)
-            src = wr_raw[G][:].rearrange("p j (r t e) -> p t r j e", t=4, e=4)[:, t]
-            copy_on(engine, dst, src)
+        def weave_wr(engine, G, lo, hi):
+            dst = w_stage[G % 2][:].rearrange("p (t r e j) -> p t r j e", t=4, e=4, j=4)
+            src = wr_raw[G][:].rearrange("p j (r t e) -> p t r j e", t=4, e=4)
+            copy_on(engine, dst[:, lo:hi], src[:, lo:hi])
 
-        def weave(dst, src, engine, lo=0, hi=W):
-            copy_on(engine, dst[:, PACK * lo:PACK * hi].rearrange("p (c i t) -> p c t i", i=4, t=PACK),
-                    src[:, :, lo:hi].rearrange("p t (c i) -> p c t i", i=4))
+        def weave(engine, dst, src, lo, hi):
+            copy_on(engine, dst[:, lo * W:hi * W].rearrange("p (c i t) -> p c t i", i=4, t=PACK),
+                    src[:, :, lo * P:hi * P].rearrange("p t (c i) -> p c t i", i=4))
 
-        def cam_pass(bank, h, G, t, g):
-            codes, scales = act_q[h * chunks + g]
-            nc.tensor.matmul_mx(out=bank[:], lhsT=wc_codes[G][:, t, g, :].bitcast(E2M1), lhsT_scale=wc_sc[G][:, t, g, :],
-                                rhs=codes[:].bitcast(E4M3), rhs_scale=scales[:], start=(g == 0), stop=(g == CAM_PASSES - 1))
+        def weave_wo(engine, G, lo, hi):
+            weave(engine, wo_stage[G], wo_raw[G], lo, hi)
 
-        def gate_of(h, G, t):
-            bank = banks.pop(0)
-            codes, scales = act_q[h * chunks + RADAR]
-            cols = slice(t * P, (t + 1) * P)
-            nc.tensor.matmul_mx(out=bank[:], lhsT=wr_q[G][0][:, cols].bitcast(E4M3), lhsT_scale=wr_q[G][1][:, cols],
-                                rhs=codes[:].bitcast(E4M3), rhs_scale=scales[:], start=True, stop=True)
-            nc.scalar.activation(out=gate[t][:], in_=bank[:], func=SIGMOID)
-            banks.append(bank)
-
-        def fuse(bank, h, G, t, lo=0, hi=W):
-            nc.vector.scalar_tensor_tensor(out=h_raw[UNITS.index((h, G)) % 2][:, t, lo:hi], in0=bank[:, lo:hi], scalar=bias[:, 4 * G + t:4 * G + t + 1],
-                                           in1=gate[t][:, lo:hi], op0=ADD, op1=MULT)
-            if hi == W:
-                banks.append(bank)
-
-        def cam_group(h, G, t):
-            bank = banks.pop(0)
-            for g in range(CAM_PASSES):
-                cam_pass(bank, h, G, t, g)
-            return bank
-
-        def cam_round(acc, h, g):
-            for t in range(PACK):
-                cam_pass(acc[t], h, 0, t, g)
-
-        def head_pass(bank, h, i, G):
-            codes, scales = h_q[h * GROUPS + G]
-            cols = slice(i * P, (i + 1) * P)
-            nc.tensor.matmul_mx(out=bank[:], lhsT=codes[:, cols].bitcast(E5M2), lhsT_scale=scales[:, cols],
-                                rhs=wo_q[G][0][:].bitcast(E4M3), rhs_scale=wo_q[G][1][:],
-                                start=(G == 0), stop=(G == GROUPS - 1))
-
-        def store(bank, h, i, engine):
-            copy_on(engine, result[h * TILES + i][:], bank[:])
-            banks.append(bank)
-            row = h * W + i * P
-            nc.sync.dma_start(out=out[row:row + P, :], in_=result[h * TILES + i][:])
-
-        S, V = nc.scalar, nc.vector
-
-        def weave_h(n, engine=V, lo=0, hi=W):
-            weave(h_stage[n % 2], h_raw[n % 2], engine, lo, hi)
+        def weave_h(engine, n, lo, hi):
+            weave(engine, h_stage[n], h_raw[n], lo, hi)
 
         def quantise_h(n, lo=0, hi=W):
             h, G = UNITS[n]
-            quantise(h_q[h * GROUPS + G], h_stage[n % 2], E5M2, lo, hi)
-
-        def head_tile(h, i):
-            bank = banks.pop(0)
-            for G in range(GROUPS):
-                head_pass(bank, h, i, G)
-            store(bank, h, i, S)
-
-        def weave_wo(G, engine, lo=0, hi=W):
-            weave(w_stage[(G + 1) % 2], wo_raw[G], engine, lo, hi)
+            quantise(h_q[h * GROUPS + G], h_stage[n], E5M2, lo, hi)
 
         def quantise_wo(G):
-            quantise(wo_q[G], w_stage[(G + 1) % 2], E4M3)
+            quantise(wo_q[G], wo_stage[G], E4M3)
 
         def quantise_wr(G):
             quantise(wr_q[G], w_stage[G % 2], E4M3)
 
-        load_act(0, 0, 0, 2)
-        load_act(0, 0, 2, 4)
-        load_act(0, 1)
-        nc.vector.memset(sc_first[:], 0)
-        nc.vector.memset(warm[:, 0:1], 0.0)
-        nc.vector.memset(b_rows[:], 0.0)
-        nc.vector.memset(sc_rest[:], 0)
-        make_identity(nc, ident[:])
-        nc.scalar.activation(out=warm[:, 1:2], in_=warm[:, 0:1], func=SIGMOID)
-        load_scales(nc.sync, sc_first, 0, 128)
-        load_wc(0, 0, 2)
-        load_act(0, 2)
-        load_wc(0, 2, 4)
-        load_act(0, RADAR)
-        load_bias()
-        load_wr(0)
-        load_act(0, 3)
-        load_act(1, 0)
-        load_act(1, 1)
-        load_wc(1)
-        load_scales(nc.sync, sc_rest, 128, 384)
-        load_act(1, 2)
-        load_wr(1)
-        load_act(1, RADAR)
-        load_wc(2)
-        load_act(1, 3)
-        load_wr(2)
-        for G in range(GROUPS):
-            load_wo(G)
-
-        acc = [banks.pop() for t in range(PACK)]
-        pair = turn(0, 0)
-        unload(0, 0, pair, 0, S)
-        unload(0, 0, pair, 1, V)
-        pair = turn(0, 1)
-        order_scales(0)
-        quantise_act(0, 0)
-        order_wc(0, 0, 2)
-        unload(0, 1, pair, 0, S)
-        unload(0, 1, pair, 1, S)
-        cam_round(acc, 0, 0)
-        quantise_act(0, 1)
-        pair = turn(0, 2)
-        unload(0, 2, pair, 0, S)
-        order_wc(0, 2, 4)
-        unload(0, 2, pair, 1, V)
-        nc.vector.tensor_copy(out=b_rows32[:], in_=b_rows[:])
-        quantise_act(0, 2)
-        cam_round(acc, 0, 1)
-        pair = turn(0, RADAR)
-        bank = banks.pop(0)
-        nc.tensor.transpose(bank[:, 0:P], b_rows32[:], ident[:])
-        unload(0, RADAR, pair, 0, S)
-        unload(0, RADAR, pair, 1, S)
-        nc.scalar.copy(out=bias[:], in_=bank[:, 0:16])
-        banks.append(bank)
-        cam_round(acc, 0, 2)
-        for t in range(PACK):
-            weave_wr(0, t, V)
-        quantise_act(0, RADAR)
-        quantise_wr(0)
-        pair = turn(0, 3)
-        unload(0, 3, pair, 0, S)
-        unload(0, 3, pair, 1, V)
-        gate_of(0, 0, 0)
-        gate_of(0, 0, 1)
-        pair = turn(1, 0)
-        quantise_act(0, 3)
-        unload(1, 0, pair, 0, S)
-        unload(1, 0, pair, 1, V)
-        gate_of(0, 0, 2)
-        gate_of(0, 0, 3)
-        cam_round(acc, 0, 3)
-        quantise_act(1, 0)
-
-        pair = turn(1, 1)
-        unload(1, 1, pair, 0, S)
-        unload(1, 1, pair, 1, S)
-        spare = list(banks)
-        for t in range(PACK):
-            fuse(acc[t], 0, 0, t)
-        banks.clear()
-        banks.extend(spare)
-        quantise_act(1, 1)
-        cam_round(acc, 1, 0)
-        pair = turn(1, 2)
-        unload(1, 2, pair, 0, S)
-        unload(1, 2, pair, 1, S)
-        weave_h(0)
-        order_wc(1)
-        quantise_act(1, 2)
-        weave_wr(1, 0, S)
-        weave_wr(1, 1, S)
-        cam_round(acc, 1, 1)
-        pair = turn(1, RADAR)
-        unload(1, RADAR, pair, 0, S)
-        unload(1, RADAR, pair, 1, S)
-        quantise_h(0)
-        order_scales(1)
-        weave_wr(1, 3, V)
-        quantise_act(1, RADAR)
-        weave_wr(1, 2, S)
-        cam_round(acc, 1, 2)
-        pair = turn(1, 3)
-        unload(1, 3, pair, 0, S)
-        order_wc(2)
-        unload(1, 3, pair, 1, V)
-        quantise_wr(1)
-        quantise_act(1, 3)
-        order_scales(2)
-        gate_of(1, 0, 0)
-        gate_of(1, 0, 1)
-        ahead = cam_group(0, 1, 0)
-        gate_of(1, 0, 2)
-        weave_wr(2, 0, V)
-        weave_wr(2, 1, V)
-        cam_pass(acc[0], 1, 0, 0, 3)
-        cam_pass(acc[1], 1, 0, 1, 3)
-        gate_of(1, 0, 3)
-        cam_pass(acc[2], 1, 0, 2, 3)
-        cam_pass(acc[3], 1, 0, 3, 3)
-        for t in range(PACK):
-            fuse(acc[t], 1, 0, t)
-
-        side = {
-            (2, 0): [lambda: weave_wr(2, 2, S), lambda: weave_wr(2, 3, S)],
-            (2, 1): [lambda: quantise_wr(2), lambda: weave_wo(0, S, 0, 128)],
-            (2, 2): [lambda: weave_wo(0, S, 128, 256)],
-            (2, 3): [lambda: weave_wo(0, S, 256, 384), lambda: weave_wo(0, V, 384, 512)],
-            (3, 0): [lambda: weave_wo(1, S, 0, 128), lambda: quantise_wo(0)],
-            (3, 1): [lambda: weave_wo(1, S, 128, 256)],
-            (3, 2): [lambda: weave_wo(1, S, 256, 384), lambda: weave_wo(1, V, 384, 512)],
-            (3, 3): [lambda: weave_wo(2, S, 0, 128), lambda: quantise_wo(1)],
-            (4, 0): [lambda: weave_wo(2, S, 128, 256)],
-            (4, 1): [lambda: weave_wo(2, S, 256, 384), lambda: weave_wo(2, V, 384, 512)],
-            (4, 2): [lambda: quantise_wo(2)],
-            (5, 0): [lambda: head_tile(0, 0)],
-            (5, 1): [lambda: head_tile(0, 1)],
-            (5, 2): [lambda: head_tile(0, 2)],
-        }
-        last = len(UNITS) - 1
-        for n in range(2, last + 1):
+        def cam_pass(bank, n, t, g):
             h, G = UNITS[n]
-            for t in range(PACK):
-                if n == 2:
-                    bank = ahead if t == 0 else cam_group(h, G, t)
-                    gate_of(h, G, t)
-                else:
-                    gate_of(h, G, t)
-                    bank = cam_group(h, G, t)
-                for job in side.get((n, t), []):
-                    job()
-                if (n, t) == (last, PACK - 1):
-                    break
-                fuse(bank, h, G, t)
-                if t == 0:
-                    weave_h(n - 1)
-                if t == 1:
-                    quantise_h(n - 1)
+            codes, scales = act_q[h * chunks + g]
+            nc.tensor.matmul_mx(out=bank[:], lhsT=wc_codes[G][:, t, g, :].bitcast(E2M1), lhsT_scale=wc_sc[G][:, t, g, :],
+                                rhs=codes[:].bitcast(E4M3), rhs_scale=scales[:], start=(g == 0), stop=(g == CAM_PASSES - 1))
 
-        early = banks.pop(0)
-        for g in range(GROUPS):
-            head_pass(early, 0, 3, g)
-        acc = [banks.pop(0) for i in range(TILES)]
-        fuse(bank, h, G, t, 0, P)
-        fuse(bank, h, G, t, P, 2 * P)
-        weave_h(last, V, 0, P)
-        weave_h(last, S, P, 2 * P)
-        fuse(bank, h, G, t, 2 * P, 4 * P)
-        quantise_h(last, 0, P)
-        weave_h(last, V, 2 * P, 3 * P)
-        quantise_h(last, P, 2 * P)
-        store(early, 0, 3, S)
-        weave_h(last, V, 3 * P, 4 * P)
-        quantise_h(last, 2 * P, 3 * P)
-        for G in range(GROUPS - 1):
-            head_pass(acc[0], 1, 0, G)
-        for G in range(GROUPS - 1):
-            head_pass(acc[1], 1, 1, G)
-        head_pass(acc[0], 1, 0, 2)
-        head_pass(acc[1], 1, 1, 2)
-        quantise_h(last, 3 * P, 4 * P)
-        for i in (2, 3):
-            for G in range(GROUPS):
-                head_pass(acc[i], 1, i, G)
-        for i in range(TILES):
-            store(acc[i], 1, i, S if i % 2 == 0 else V)
+        def cam_round(n, g, lo=0, hi=PACK):
+            for t in range(lo, hi):
+                cam_pass(take(("cam", n, t)) if g == 0 else held[("cam", n, t)], n, t, g)
+
+        def cam_group(n, t):
+            bank = take(("cam", n, t))
+            for g in range(CAM_PASSES):
+                cam_pass(bank, n, t, g)
+
+        def radar_pass(n, t):
+            h, G = UNITS[n]
+            codes, scales = act_q[h * chunks + RADAR]
+            cols = slice(t * P, (t + 1) * P)
+            nc.tensor.matmul_mx(out=take(("radar", n, t))[:], lhsT=wr_q[G][0][:, cols].bitcast(E4M3), lhsT_scale=wr_q[G][1][:, cols],
+                                rhs=codes[:].bitcast(E4M3), rhs_scale=scales[:], start=True, stop=True)
+
+        def sigmoid(n, t):
+            nc.scalar.activation(out=gate[(PACK * n + t) % len(gate)][:], in_=held[("radar", n, t)][:], func=SIGMOID)
+            give(("radar", n, t))
+
+        def fuse(n, t, lo=0, hi=W):
+            col = PACK * UNITS[n][1] + t
+            nc.vector.scalar_tensor_tensor(out=h_raw[n][:, t, lo:hi], in0=held[("cam", n, t)][:, lo:hi], scalar=bias[:, col:col + 1],
+                                           in1=gate[(PACK * n + t) % len(gate)][:, lo:hi], op0=ADD, op1=MULT)
+            if hi == W:
+                give(("cam", n, t))
+
+        def head_passes(h, i, lo, hi):
+            bank = take(("head", h, i)) if lo == 0 else held[("head", h, i)]
+            cols = slice(i * P, (i + 1) * P)
+            for G in range(lo, hi):
+                codes, scales = h_q[h * GROUPS + G]
+                nc.tensor.matmul_mx(out=bank[:], lhsT=codes[:, cols].bitcast(E5M2), lhsT_scale=scales[:, cols],
+                                    rhs=wo_q[G][0][:].bitcast(E4M3), rhs_scale=wo_q[G][1][:],
+                                    start=(G == 0), stop=(G == GROUPS - 1))
+
+        def copy_out(engine, h, i, lo=0, hi=W):
+            copy_on(engine, result[h * TILES + i][:, lo:hi], held[("head", h, i)][:, lo:hi])
+            if hi == W:
+                give(("head", h, i))
+
+        def store(h, i, lo=0, hi=W):
+            rows = out[h * W:(h + 1) * W, lo:hi].rearrange("(p i) n -> p i n", i=TILES)
+            nc.sync.dma_start(out=rows[:, i, :], in_=result[h * TILES + i][:, lo:hi])
+
+        def widen_bias():
+            nc.vector.tensor_copy(out=b_rows32[:], in_=b_rows[:])
+
+        def turn_bias():
+            nc.tensor.transpose(take("bias")[:, 0:P], b_rows32[:], ident[:])
+
+        def unload_bias(engine):
+            copy_on(engine, bias[:], held["bias"][:, 0:16])
+            give("bias")
+
+        load_cam(0, 0, 0, 1)
+        nc.vector.memset(warm[:, 0:1], 0.0)
+        nc.scalar.activation(out=warm[:, 1:2], in_=warm[:, 0:1], func=SIGMOID)
+        nc.vector.memset(sc_first[:], 0)
+        make_identity(nc, ident[:])
+        load_cam(0, 0, 1, 2)
+        load_cam(0, 0, 2, 4)
+        load_cam(0, 1, 0, 2)
+        nc.vector.memset(b_rows[:], 0.0)
+        load_scales(nc.sync, sc_first, 0, 128)
+        nc.vector.memset(sc_rest[:], 0)
+        load_wc(0, 0, 2)
+        load_cam(0, 1, 2, 4)
+        turn(0, 0, 0)
+        split(V, 0, 1, 0)
+        turn(0, 1, 0)
+        unload(S, 0, 0, 0)
+        load_radar(0)
+        turn(0, 0, 1)
+        unload(S, 0, 1, 0)
+        quantise_act(0, 0, 0, 256)
+        turn(0, 1, 1)
+        unload(S, 0, 0, 1)
+        load_wc(0, 2, 4)
+        split(V, 0, 2, 0)
+        load_wr(0)
+        load_bias()
+        split(S, 0, 3, 0)
+        order_scales(0)
+        turn(0, 2, 0)
+        quantise_act(0, 0, 256, 512)
+        load_cam(1, 0, 0, 2)
+        turn(0, 3, 0)
+        unload(S, 0, 2, 0)
+        order_wc(0, 0, 2)
+        unload(V, 0, 1, 1)
+        cam_round(0, 0, 0, 4)
+        unload(S, 0, 3, 0)
+        load_cam(1, 0, 2, 4)
+        quantise_act(0, 2, 0, 256)
+        split(S, 0, 3, 1)
+        quantise_act(0, 1, 256, 512)
+        split(V, 0, 2, 1)
+        quantise_act(0, 1, 0, 256)
+        load_cam(1, 1, 0, 2)
+        split(S, 0, 4, 0)
+        turn(0, 2, 1)
+        quantise_act(0, 3, 0, 256)
+        turn(0, 3, 1)
+        split(S, 0, 4, 1)
+        load_cam(1, 1, 2, 4)
+        cam_round(0, 1, 0, 4)
+        unload(V, 0, 2, 1)
+        unload(S, 0, 3, 1)
+        quantise_act(0, 2, 256, 512)
+        load_wc(1)
+        weave_wr(S, 0, 0, 1)
+        turn(0, 4, 0)
+        load_scales(nc.sync, sc_rest, 128, 384)
+        weave_wr(V, 0, 1, 2)
+        order_wc(0, 2, 4)
+        turn(0, 4, 1)
+        widen_bias()
+        unload(S, 0, 4, 0)
+        weave_wr(V, 0, 2, 3)
+        cam_round(0, 2, 0, 4)
+        split(V, 1, 1, 0)
+        unload(S, 0, 4, 1)
+        weave_wr(V, 0, 3, 4)
+        turn_bias()
+        quantise_act(0, 4)
+        turn(1, 0, 0)
+        load_radar(1)
+        split(S, 1, 1, 1)
+        unload_bias(V)
+        turn(1, 0, 1)
+        quantise_act(0, 3, 256, 512)
+        quantise_wr(0)
+        unload(S, 1, 0, 0)
+        turn(1, 1, 0)
+        load_wr(1)
+        cam_round(0, 3, 0, 2)
+        unload(S, 1, 0, 1)
+        split(V, 1, 2, 0)
+        unload(V, 1, 1, 0)
+        radar_pass(0, 0)
+        split(S, 1, 3, 0)
+        turn(1, 1, 1)
+        load_wc(2)
+        split(V, 1, 2, 1)
+        sigmoid(0, 0)
+        radar_pass(0, 1)
+        split(V, 1, 3, 1)
+        radar_pass(0, 2)
+        quantise_act(1, 0)
+        cam_round(0, 3, 2, 4)
+        sigmoid(0, 1)
+        fuse(0, 0)
+        load_wr(2)
+        turn(1, 2, 0)
+        unload(S, 1, 1, 1)
+        load_wo(0)
+        fuse(0, 1)
+        sigmoid(0, 2)
+        cam_round(1, 0, 0, 2)
+        order_wc(1)
+        unload(S, 1, 2, 0)
+        turn(1, 2, 1)
+        fuse(0, 2)
+        load_wo(1)
+        turn(1, 4, 0)
+        unload(S, 1, 2, 1)
+        turn(1, 4, 1)
+        quantise_act(1, 1)
+        unload(S, 1, 4, 0)
+        turn(1, 3, 0)
+        quantise_act(1, 2)
+        turn(1, 3, 1)
+        unload(S, 1, 4, 1)
+        radar_pass(0, 3)
+        order_scales(2)
+        cam_round(1, 0, 2, 4)
+        unload(S, 1, 3, 1)
+        quantise_act(1, 4)
+        cam_round(1, 1, 0, 4)
+        sigmoid(0, 3)
+        order_wc(2)
+        weave_wr(S, 1, 1, 2)
+        fuse(0, 3)
+        cam_round(1, 2, 0, 4)
+        unload(S, 1, 3, 0)
+        order_scales(1)
+        load_wo(2)
+        weave_wr(S, 1, 0, 1)
+        quantise_act(1, 3)
+        radar_pass(1, 0)
+        radar_pass(1, 1)
+        weave_wr(V, 1, 2, 3)
+        radar_pass(1, 2)
+        sigmoid(1, 0)
+        cam_group(2, 0)
+        weave_wr(V, 1, 3, 4)
+        sigmoid(1, 1)
+        weave_wr(V, 2, 3, 4)
+        quantise_wr(1)
+        sigmoid(1, 2)
+        radar_pass(1, 3)
+        cam_round(1, 3, 0, 2)
+        weave_wr(V, 2, 1, 2)
+        sigmoid(1, 3)
+        radar_pass(2, 0)
+        fuse(1, 0)
+        cam_round(1, 3, 2, 4)
+        weave_wr(S, 2, 0, 1)
+        fuse(1, 1)
+        cam_group(2, 1)
+        sigmoid(2, 0)
+        fuse(1, 3)
+        weave_wr(S, 2, 2, 3)
+        fuse(1, 2)
+        cam_group(2, 2)
+        weave_wo(S, 2, 0, 2)
+        quantise_wr(2)
+        fuse(2, 0)
+        radar_pass(2, 1)
+        radar_pass(2, 2)
+        cam_group(2, 3)
+        weave_wo(V, 0, 2, 4)
+        sigmoid(2, 1)
+        sigmoid(2, 2)
+        fuse(2, 1)
+        radar_pass(2, 3)
+        weave_wo(S, 0, 0, 2)
+        weave_wo(V, 1, 2, 4)
+        radar_pass(3, 0)
+        cam_group(3, 0)
+        fuse(2, 2)
+        sigmoid(3, 0)
+        weave_wo(V, 1, 0, 2)
+        radar_pass(3, 1)
+        cam_group(3, 1)
+        sigmoid(2, 3)
+        fuse(3, 0)
+        sigmoid(3, 1)
+        fuse(2, 3)
+        radar_pass(3, 2)
+        weave_h(S, 0, 2, 4)
+        cam_group(3, 2)
+        fuse(3, 1)
+        weave_h(V, 2, 2, 4)
+        sigmoid(3, 2)
+        radar_pass(3, 3)
+        quantise_wo(1)
+        cam_group(3, 3)
+        weave_h(S, 2, 0, 2)
+        fuse(3, 2)
+        radar_pass(4, 0)
+        quantise_wo(0)
+        cam_group(4, 0)
+        sigmoid(4, 0)
+        quantise_h(2)
+        sigmoid(3, 3)
+        weave_h(V, 0, 0, 2)
+        radar_pass(4, 1)
+        cam_group(4, 1)
+        weave_wo(S, 2, 2, 4)
+        fuse(4, 0)
+        fuse(3, 3)
+        radar_pass(4, 2)
+        sigmoid(4, 1)
+        cam_group(4, 2)
+        quantise_wo(2)
+        sigmoid(4, 2)
+        weave_h(V, 3, 0, 2)
+        radar_pass(4, 3)
+        weave_h(S, 3, 2, 4)
+        cam_group(4, 3)
+        quantise_h(0)
+        fuse(4, 1)
+        sigmoid(4, 3)
+        radar_pass(5, 0)
+        quantise_h(3)
+        cam_group(5, 0)
+        weave_h(S, 1, 0, 2)
+        fuse(4, 3)
+        weave_h(V, 1, 2, 4)
+        head_passes(0, 0, 0, 3)
+        sigmoid(5, 0)
+        fuse(4, 2)
+        radar_pass(5, 1)
+        cam_group(5, 1)
+        copy_out(S, 0, 0)
+        fuse(5, 0)
+        sigmoid(5, 1)
+        quantise_h(1)
+        store(0, 0)
+        head_passes(0, 1, 0, 3)
+        weave_h(S, 4, 0, 2)
+        fuse(5, 1)
+        radar_pass(5, 2)
+        weave_h(V, 4, 2, 4)
+        cam_group(5, 2)
+        copy_out(S, 0, 1)
+        quantise_h(4)
+        sigmoid(5, 2)
+        store(0, 1)
+        head_passes(0, 2, 0, 3)
+        fuse(5, 2)
+        radar_pass(5, 3)
+        cam_group(5, 3)
+        copy_out(V, 0, 2)
+        sigmoid(5, 3)
+        store(0, 2)
+        head_passes(0, 3, 0, 3)
+        fuse(5, 3, 0, 128)
+        fuse(5, 3, 128, 256)
+        head_passes(1, 0, 0, 2)
+        weave_h(V, 5, 0, 1)
+        weave_h(S, 5, 1, 2)
+        fuse(5, 3, 256, 384)
+        head_passes(1, 1, 0, 2)
+        quantise_h(5, 0, 128)
+        copy_out(S, 0, 3)
+        head_passes(1, 2, 0, 2)
+        quantise_h(5, 128, 256)
+        weave_h(V, 5, 2, 3)
+        head_passes(1, 0, 2, 3)
+        fuse(5, 3, 384, 512)
+        store(0, 3)
+        head_passes(1, 1, 2, 3)
+        quantise_h(5, 256, 384)
+        weave_h(S, 5, 3, 4)
+        copy_out(V, 1, 0)
+        head_passes(1, 2, 2, 3)
+        copy_out(S, 1, 1)
+        head_passes(1, 3, 0, 2)
+        quantise_h(5, 384, 512)
+        store(1, 0)
+        copy_out(V, 1, 2)
+        head_passes(1, 3, 2, 3)
+        store(1, 1)
+        store(1, 2)
+        copy_out(V, 1, 3, 0, 256)
+        store(1, 3, 0, 256)
+        copy_out(V, 1, 3, 256, 512)
+        store(1, 3, 256, 512)

@@ -26,9 +26,8 @@ CAM_PASSES = KC // W
 RADAR = CAM_PASSES
 GROUPS = F // W
 TILES = W // P
-ORDER = [(0, 0), (0, 1), (0, 2), (0, 3), (0, RADAR), (1, 0), (1, 1), (1, 2), (1, RADAR), (1, 3)]
-SPLIT = [(0, 1, 0), (0, 2, 0), (0, 3, 0), (0, 3, 1), (0, 2, 1), (0, 4, 0), (0, 4, 1), (1, 1, 0), (1, 1, 1), (1, 2, 0), (1, 3, 0), (1, 2, 1), (1, 3, 1)]
-UNITS = [(0, 0), (1, 0), (0, 1), (0, 2), (1, 1), (1, 2)]
+ORDER = [(0, 0), (0, 1), (0, 2), (0, 3), (0, RADAR), (1, 0), (1, 1), (1, 2), (1, 3), (1, RADAR)]
+UNITS = [(0, 0), (0, 1), (0, 2), (1, 0), (1, 1), (1, 2)]
 
 
 def tile_camera_radar_gated_fusion_s9_kernel(tc, cam, wc_words, wc_scales, b, radar, wr, wo, out):
@@ -51,9 +50,9 @@ def tile_camera_radar_gated_fusion_s9_kernel(tc, cam, wc_words, wc_scales, b, ra
         banks = [ps.tile([P, W], F32, name="bank%d" % i) for i in range(8)]
         ident = sb.tile([P, P], F32, name="ident")
         warm = sb.tile([P, 8], F32, name="warm")
-        b_rows = sb.tile([P, P], BF16, name="b_rows")
-        b_rows32 = sb.tile([P, P], F32, name="b_rows32")
-        bias = sb.tile([P, 16], F32, name="bias")
+        b_rows = sb.tile([P, W], BF16, name="b_rows")
+        b_rows32 = sb.tile([P, PACK, P], F32, name="b_rows32")
+        bias = sb.tile([P, PACK, 4], F32, name="bias")
         chunks = CAM_PASSES + 1
         cam_raw = tiles("cam_raw", HALVES * 2, [P, TILES, 2 * W], BF16)
         radar_raw = tiles("radar_raw", HALVES, [P, TILES, W], BF16)
@@ -74,7 +73,7 @@ def tile_camera_radar_gated_fusion_s9_kernel(tc, cam, wc_words, wc_scales, b, ra
         gate = tiles("gate", 6, [P, W], F32)
         h_raw = [reused[n].rearrange("p (t m) -> p t m", t=PACK) for n in range(6)]
         h_own = tiles("h_stage", 2, [P, PACK * W], BF16)
-        h_stage = [h_own[0], act_stage[1], h_own[1], act_stage[2], act_stage[0], h_own[0]]
+        h_stage = [h_own[0], h_own[1], h_own[0], act_stage[1], act_stage[2], act_stage[0]]
         wo_stage = [radar_raw[0][:].rearrange("p i k -> p (i k)"), reused[6], reused[7]]
         h_q = quantised("h", HALVES * GROUPS)
         result = tiles("result", HALVES * TILES, [P, W], F32)
@@ -82,6 +81,10 @@ def tile_camera_radar_gated_fusion_s9_kernel(tc, cam, wc_words, wc_scales, b, ra
         def load_cam(h, d, lo, hi):
             rows = cam[h * W:(h + 1) * W, 2 * W * d:2 * W * (d + 1)].rearrange("(p i) k -> p i k", i=TILES)
             nc.sync.dma_start(out=cam_raw[2 * h + d][:, lo:hi, :], in_=rows[:, lo:hi, :])
+
+        def load_first(c, lo, hi):
+            rows = cam[0:W, c * W:(c + 1) * W].rearrange("(p i) k -> p i k", i=TILES)
+            nc.sync.dma_start(out=h_raw[c][:, lo:hi, :], in_=rows[:, lo:hi, :])
 
         def load_radar(h):
             nc.sync.dma_start(out=radar_raw[h][:], in_=radar[h * W:(h + 1) * W, :].rearrange("(p i) k -> p i k", i=TILES))
@@ -105,9 +108,7 @@ def tile_camera_radar_gated_fusion_s9_kernel(tc, cam, wc_words, wc_scales, b, ra
                 nc.sync.dma_start(out=wo_raw[G][e:P:4, :, :], in_=src[e])
 
         def load_bias():
-            src = b.rearrange("(G r t e) -> G t r e", G=GROUPS, t=4, e=4)
-            for G in range(GROUPS):
-                nc.sync.dma_start(out=b_rows[4 * G:4 * G + 4, :].rearrange("t (r e) -> t r e", e=4), in_=src[G])
+            nc.scalar.dma_start(out=b_rows[0:GROUPS, :], in_=b.rearrange("(G f) -> G f", G=GROUPS))
 
         S, V = nc.scalar, nc.vector
         held = {}
@@ -127,18 +128,24 @@ def tile_camera_radar_gated_fusion_s9_kernel(tc, cam, wc_words, wc_scales, b, ra
 
         def halves(h, c):
             raw = radar_raw[h][:] if c == RADAR else cam_raw[2 * h + c // 2][:, :, (c % 2) * W:(c % 2 + 1) * W]
+            if h == 0 and c < 2:
+                raw = h_raw[c]
             return raw.bitcast(F32).rearrange("p i (w u) -> p i u w", u=2)
 
         def split(engine, h, c, j):
-            copy_on(engine, act_split[SPLIT.index((h, c, j)) % 6][:], halves(h, c)[:, 2 * j:2 * j + 2])
+            held[("split", h, c, j)] = act_split.pop(0)
+            copy_on(engine, held[("split", h, c, j)][:], halves(h, c)[:, 2 * j:2 * j + 2])
 
         def turn(h, c, j):
-            words = act_split[SPLIT.index((h, c, j)) % 6][:] if (h, c, j) in SPLIT else halves(h, c)[:, 2 * j:2 * j + 2]
+            is_split = ("split", h, c, j) in held
+            words = held[("split", h, c, j)][:] if is_split else halves(h, c)[:, 2 * j:2 * j + 2]
             bank = take(("turn", h, c, j))
             for i in range(2):
                 for u in range(2):
                     col = (2 * i + u) * P
                     nc.tensor.transpose(bank[:, col:col + P], words[:, i, u, :], ident[:])
+            if is_split:
+                act_split.append(held[("split", h, c, j)])
 
         def unload(engine, h, c, j):
             stage = act_stage[ORDER.index((h, c)) % 3][:].bitcast(F32)
@@ -164,7 +171,11 @@ def tile_camera_radar_gated_fusion_s9_kernel(tc, cam, wc_words, wc_scales, b, ra
         def weave_wr(engine, G, lo, hi):
             dst = w_stage[G % 2][:].rearrange("p (t r e j) -> p t r j e", t=4, e=4, j=4)
             src = wr_raw[G][:].rearrange("p j (r t e) -> p t r j e", t=4, e=4)
-            copy_on(engine, dst[:, lo:hi], src[:, lo:hi])
+            if engine is nc.scalar:
+                for t in range(lo, hi):
+                    nc.scalar.copy(out=dst[:, t], in_=src[:, t])
+            else:
+                nc.vector.tensor_copy(out=dst[:, lo:hi], in_=src[:, lo:hi])
 
         def weave(engine, dst, src, lo, hi):
             copy_on(engine, dst[:, lo * W:hi * W].rearrange("p (c i t) -> p c t i", i=4, t=PACK),
@@ -213,8 +224,8 @@ def tile_camera_radar_gated_fusion_s9_kernel(tc, cam, wc_words, wc_scales, b, ra
             give(("radar", n, t))
 
         def fuse(n, t, lo=0, hi=W):
-            col = PACK * UNITS[n][1] + t
-            nc.vector.scalar_tensor_tensor(out=h_raw[n][:, t, lo:hi], in0=held[("cam", n, t)][:, lo:hi], scalar=bias[:, col:col + 1],
+            G = UNITS[n][1]
+            nc.vector.scalar_tensor_tensor(out=h_raw[n][:, t, lo:hi], in0=held[("cam", n, t)][:, lo:hi], scalar=bias[:, t, G:G + 1],
                                            in1=gate[(PACK * n + t) % len(gate)][:, lo:hi], op0=ADD, op1=MULT)
             if hi == W:
                 give(("cam", n, t))
@@ -238,296 +249,287 @@ def tile_camera_radar_gated_fusion_s9_kernel(tc, cam, wc_words, wc_scales, b, ra
             nc.sync.dma_start(out=rows[:, i, :], in_=result[h * TILES + i][:, lo:hi])
 
         def widen_bias():
-            nc.vector.tensor_copy(out=b_rows32[:], in_=b_rows[:])
+            nc.vector.tensor_copy(out=b_rows32[:].rearrange("G t (r e) -> G t r e", e=4),
+                                  in_=b_rows[:].rearrange("G (r t e) -> G t r e", t=4, e=4))
 
         def turn_bias():
-            nc.tensor.transpose(take("bias")[:, 0:P], b_rows32[:], ident[:])
+            bank = take("bias")
+            for t in range(PACK):
+                nc.tensor.transpose(bank[:, t * P:(t + 1) * P], b_rows32[:, t, :], ident[:])
 
         def unload_bias(engine):
-            copy_on(engine, bias[:], held["bias"][:, 0:16])
+            copy_on(engine, bias[:], held["bias"][:].rearrange("p (t G) -> p t G", t=PACK)[:, :, 0:4])
             give("bias")
 
-        load_cam(0, 0, 0, 1)
-        nc.vector.memset(warm[:, 0:1], 0.0)
-        nc.scalar.activation(out=warm[:, 1:2], in_=warm[:, 0:1], func=SIGMOID)
-        nc.vector.memset(sc_first[:], 0)
-        make_identity(nc, ident[:])
-        load_cam(0, 0, 1, 2)
-        load_cam(0, 0, 2, 4)
-        load_cam(0, 1, 0, 2)
+        load_first(0, 0, 2)
         nc.vector.memset(b_rows[:], 0.0)
-        load_scales(nc.sync, sc_first, 0, 128)
-        nc.vector.memset(sc_rest[:], 0)
-        load_wc(0, 0, 2)
-        load_cam(0, 1, 2, 4)
-        turn(0, 0, 0)
-        split(V, 0, 1, 0)
-        turn(0, 1, 0)
-        unload(S, 0, 0, 0)
-        load_radar(0)
-        turn(0, 0, 1)
-        unload(S, 0, 1, 0)
-        quantise_act(0, 0, 0, 256)
-        turn(0, 1, 1)
-        unload(S, 0, 0, 1)
-        load_wc(0, 2, 4)
-        split(V, 0, 2, 0)
-        load_wr(0)
+        make_identity(nc, ident[:])
+        load_first(0, 2, 4)
+        load_wc(0, 0, 1)
+        load_first(1, 0, 4)
+        nc.vector.memset(warm[:, 0:1], 0.0)
+        nc.vector.memset(sc_first[:], 0)
         load_bias()
-        split(S, 0, 3, 0)
-        order_scales(0)
-        turn(0, 2, 0)
-        quantise_act(0, 0, 256, 512)
-        load_cam(1, 0, 0, 2)
-        turn(0, 3, 0)
-        unload(S, 0, 2, 0)
-        order_wc(0, 0, 2)
-        unload(V, 0, 1, 1)
-        cam_round(0, 0, 0, 4)
-        unload(S, 0, 3, 0)
-        load_cam(1, 0, 2, 4)
-        quantise_act(0, 2, 0, 256)
-        split(S, 0, 3, 1)
-        quantise_act(0, 1, 256, 512)
-        split(V, 0, 2, 1)
-        quantise_act(0, 1, 0, 256)
-        load_cam(1, 1, 0, 2)
-        split(S, 0, 4, 0)
-        turn(0, 2, 1)
-        quantise_act(0, 3, 0, 256)
-        turn(0, 3, 1)
-        split(S, 0, 4, 1)
-        load_cam(1, 1, 2, 4)
-        cam_round(0, 1, 0, 4)
-        unload(V, 0, 2, 1)
-        unload(S, 0, 3, 1)
-        quantise_act(0, 2, 256, 512)
-        load_wc(1)
-        weave_wr(S, 0, 0, 1)
-        turn(0, 4, 0)
-        load_scales(nc.sync, sc_rest, 128, 384)
-        weave_wr(V, 0, 1, 2)
-        order_wc(0, 2, 4)
-        turn(0, 4, 1)
+        nc.vector.memset(sc_rest[:], 0)
+        load_scales(nc.sync, sc_first, 0, 128)
+        nc.scalar.activation(out=warm[:, 1:2], in_=warm[:, 0:1], func=SIGMOID)
+        load_cam(0, 1, 0, 2)
+        turn(0, 0, 0)
         widen_bias()
-        unload(S, 0, 4, 0)
-        weave_wr(V, 0, 2, 3)
-        cam_round(0, 2, 0, 4)
-        split(V, 1, 1, 0)
-        unload(S, 0, 4, 1)
-        weave_wr(V, 0, 3, 4)
+        load_cam(0, 1, 2, 4)
+        turn(0, 0, 1)
+        unload(V, 0, 0, 0)
+        load_wc(0, 1, 2)
         turn_bias()
-        quantise_act(0, 4)
-        turn(1, 0, 0)
-        load_radar(1)
-        split(S, 1, 1, 1)
+        order_wc(0, 0, 1)
+        unload(S, 0, 0, 1)
         unload_bias(V)
-        turn(1, 0, 1)
-        quantise_act(0, 3, 256, 512)
-        quantise_wr(0)
-        unload(S, 1, 0, 0)
-        turn(1, 1, 0)
+        quantise_act(0, 0, 0, 256)
+        quantise_act(0, 0, 256, 512)
+        load_wc(0, 2, 4)
+        turn(0, 1, 0)
+        load_wr(0)
+        load_radar(0)
+        load_scales(nc.sync, sc_rest, 128, 384)
+        turn(0, 1, 1)
+        order_scales(0)
+        unload(V, 0, 1, 0)
+        cam_round(0, 0, 0, 4)
+        unload(S, 0, 1, 1)
+        split(V, 0, 2, 0)
+        split(S, 0, 3, 0)
+        quantise_act(0, 1)
+        split(S, 0, 2, 1)
         load_wr(1)
-        cam_round(0, 3, 0, 2)
-        unload(S, 1, 0, 1)
-        split(V, 1, 2, 0)
-        unload(V, 1, 1, 0)
-        radar_pass(0, 0)
-        split(S, 1, 3, 0)
-        turn(1, 1, 1)
-        load_wc(2)
-        split(V, 1, 2, 1)
-        sigmoid(0, 0)
-        radar_pass(0, 1)
-        split(V, 1, 3, 1)
-        radar_pass(0, 2)
-        quantise_act(1, 0)
-        cam_round(0, 3, 2, 4)
-        sigmoid(0, 1)
-        fuse(0, 0)
+        turn(0, 2, 0)
+        order_wc(0, 1, 2)
+        load_wc(1)
+        turn(0, 3, 0)
+        turn(0, 2, 1)
+        unload(S, 0, 2, 0)
+        turn(0, 3, 1)
+        unload(V, 0, 3, 0)
+        unload(S, 0, 2, 1)
+        cam_round(0, 1, 0, 4)
+        load_cam(1, 0, 2, 4)
+        weave_wr(V, 0, 2, 4)
+        weave_wr(S, 0, 0, 2)
+        quantise_act(0, 2)
         load_wr(2)
-        turn(1, 2, 0)
-        unload(S, 1, 1, 1)
-        load_wo(0)
-        fuse(0, 1)
-        sigmoid(0, 2)
-        cam_round(1, 0, 0, 2)
-        order_wc(1)
-        unload(S, 1, 2, 0)
-        turn(1, 2, 1)
-        fuse(0, 2)
-        load_wo(1)
-        turn(1, 4, 0)
-        unload(S, 1, 2, 1)
-        turn(1, 4, 1)
-        quantise_act(1, 1)
-        unload(S, 1, 4, 0)
-        turn(1, 3, 0)
-        quantise_act(1, 2)
-        turn(1, 3, 1)
-        unload(S, 1, 4, 1)
-        radar_pass(0, 3)
-        order_scales(2)
-        cam_round(1, 0, 2, 4)
-        unload(S, 1, 3, 1)
-        quantise_act(1, 4)
-        cam_round(1, 1, 0, 4)
-        sigmoid(0, 3)
-        order_wc(2)
-        weave_wr(S, 1, 1, 2)
-        fuse(0, 3)
-        cam_round(1, 2, 0, 4)
-        unload(S, 1, 3, 0)
+        turn(0, 4, 0)
+        split(V, 0, 4, 1)
+        load_cam(1, 1, 0, 2)
+        unload(S, 0, 3, 1)
+        order_wc(0, 2, 4)
+        load_cam(1, 0, 0, 2)
+        turn(0, 4, 1)
+        quantise_wr(0)
+        load_radar(1)
+        cam_round(0, 2, 0, 4)
+        unload(S, 0, 4, 0)
+        load_wc(2)
+        quantise_act(0, 3)
+        unload(S, 0, 4, 1)
         order_scales(1)
-        load_wo(2)
-        weave_wr(S, 1, 0, 1)
-        quantise_act(1, 3)
-        radar_pass(1, 0)
-        radar_pass(1, 1)
-        weave_wr(V, 1, 2, 3)
-        radar_pass(1, 2)
-        sigmoid(1, 0)
-        cam_group(2, 0)
-        weave_wr(V, 1, 3, 4)
-        sigmoid(1, 1)
-        weave_wr(V, 2, 3, 4)
+        cam_round(0, 3, 0, 2)
+        load_cam(1, 1, 2, 4)
+        weave_wr(S, 1, 0, 2)
+        quantise_act(0, 4)
+        cam_round(0, 3, 2, 4)
+        weave_wr(V, 1, 2, 4)
+        radar_pass(0, 0)
+        radar_pass(0, 1)
+        load_wo(0)
+        order_wc(1)
+        radar_pass(0, 2)
+        sigmoid(0, 0)
+        radar_pass(0, 3)
         quantise_wr(1)
-        sigmoid(1, 2)
-        radar_pass(1, 3)
-        cam_round(1, 3, 0, 2)
-        weave_wr(V, 2, 1, 2)
-        sigmoid(1, 3)
-        radar_pass(2, 0)
-        fuse(1, 0)
-        cam_round(1, 3, 2, 4)
-        weave_wr(S, 2, 0, 1)
-        fuse(1, 1)
-        cam_group(2, 1)
-        sigmoid(2, 0)
-        fuse(1, 3)
-        weave_wr(S, 2, 2, 3)
-        fuse(1, 2)
-        cam_group(2, 2)
-        weave_wo(S, 2, 0, 2)
+        sigmoid(0, 1)
+        cam_group(1, 0)
+        fuse(0, 0)
+        sigmoid(0, 2)
+        fuse(0, 1)
+        split(S, 1, 0, 1)
+        cam_group(1, 1)
+        fuse(0, 2)
+        sigmoid(0, 3)
+        weave_wr(V, 2, 2, 4)
+        radar_pass(1, 0)
+        weave_wr(S, 2, 0, 2)
+        cam_group(1, 2)
+        fuse(0, 3)
+        order_scales(2)
+        sigmoid(1, 0)
+        radar_pass(1, 1)
+        radar_pass(1, 2)
         quantise_wr(2)
-        fuse(2, 0)
+        radar_pass(1, 3)
+        sigmoid(1, 1)
+        load_wo(1)
+        cam_group(1, 3)
+        fuse(1, 0)
+        sigmoid(1, 2)
+        fuse(1, 1)
+        split(S, 1, 3, 0)
+        radar_pass(2, 0)
+        turn(1, 0, 0)
+        fuse(1, 2)
+        sigmoid(1, 3)
+        turn(1, 1, 0)
+        split(V, 1, 2, 0)
+        sigmoid(2, 0)
+        unload(V, 1, 0, 0)
         radar_pass(2, 1)
         radar_pass(2, 2)
-        cam_group(2, 3)
-        weave_wo(V, 0, 2, 4)
+        unload(S, 1, 1, 0)
+        fuse(1, 3)
+        turn(1, 0, 1)
         sigmoid(2, 1)
-        sigmoid(2, 2)
-        fuse(2, 1)
+        turn(1, 1, 1)
+        order_wc(2)
+        load_wo(2)
+        turn(1, 2, 0)
+        unload(S, 1, 0, 1)
+        weave_h(V, 0, 2, 4)
+        turn(1, 3, 0)
+        unload(S, 1, 1, 1)
         radar_pass(2, 3)
-        weave_wo(S, 0, 0, 2)
-        weave_wo(V, 1, 2, 4)
-        radar_pass(3, 0)
-        cam_group(3, 0)
-        fuse(2, 2)
-        sigmoid(3, 0)
-        weave_wo(V, 1, 0, 2)
-        radar_pass(3, 1)
-        cam_group(3, 1)
+        unload(V, 1, 2, 0)
+        cam_group(2, 0)
+        sigmoid(2, 2)
+        quantise_act(1, 0)
+        split(S, 1, 3, 1)
+        quantise_act(1, 1)
+        cam_group(2, 1)
+        unload(S, 1, 3, 0)
+        fuse(2, 0)
         sigmoid(2, 3)
-        fuse(3, 0)
-        sigmoid(3, 1)
+        turn(1, 2, 1)
+        split(V, 1, 4, 0)
+        fuse(2, 1)
+        split(S, 1, 4, 1)
+        turn(1, 3, 1)
+        turn(1, 4, 0)
+        weave_wo(V, 1, 2, 4)
+        unload(S, 1, 2, 1)
+        turn(1, 4, 1)
+        cam_group(2, 2)
+        unload(S, 1, 3, 1)
+        quantise_act(1, 2)
+        unload(S, 1, 4, 1)
+        quantise_act(1, 3)
+        cam_group(2, 3)
+        weave_wo(S, 0, 2, 4)
+        fuse(2, 2)
+        unload(V, 1, 4, 0)
+        cam_group(3, 0)
+        weave_h(S, 1, 0, 2)
         fuse(2, 3)
-        radar_pass(3, 2)
-        weave_h(S, 0, 2, 4)
+        quantise_act(1, 4)
+        cam_group(3, 1)
+        weave_h(S, 0, 0, 2)
+        weave_h(V, 1, 2, 4)
+        radar_pass(3, 0)
+        weave_wo(V, 2, 0, 2)
+        radar_pass(3, 1)
         cam_group(3, 2)
-        fuse(3, 1)
-        weave_h(V, 2, 2, 4)
-        sigmoid(3, 2)
-        radar_pass(3, 3)
-        quantise_wo(1)
-        cam_group(3, 3)
+        sigmoid(3, 0)
+        quantise_h(0)
+        sigmoid(3, 1)
+        fuse(3, 0)
+        radar_pass(3, 2)
         weave_h(S, 2, 0, 2)
-        fuse(3, 2)
-        radar_pass(4, 0)
-        quantise_wo(0)
+        radar_pass(3, 3)
+        fuse(3, 1)
+        cam_group(3, 3)
+        quantise_h(1)
+        sigmoid(3, 2)
+        weave_wo(V, 2, 2, 4)
         cam_group(4, 0)
-        sigmoid(4, 0)
-        quantise_h(2)
         sigmoid(3, 3)
-        weave_h(V, 0, 0, 2)
+        fuse(3, 2)
+        weave_wo(S, 0, 0, 2)
+        radar_pass(4, 0)
+        fuse(3, 3)
         radar_pass(4, 1)
         cam_group(4, 1)
-        weave_wo(S, 2, 2, 4)
-        fuse(4, 0)
-        fuse(3, 3)
+        quantise_wo(2)
+        sigmoid(4, 0)
+        quantise_wo(0)
         radar_pass(4, 2)
         sigmoid(4, 1)
-        cam_group(4, 2)
-        quantise_wo(2)
-        sigmoid(4, 2)
-        weave_h(V, 3, 0, 2)
         radar_pass(4, 3)
-        weave_h(S, 3, 2, 4)
-        cam_group(4, 3)
-        quantise_h(0)
+        fuse(4, 0)
+        cam_group(4, 2)
+        sigmoid(4, 2)
         fuse(4, 1)
         sigmoid(4, 3)
-        radar_pass(5, 0)
-        quantise_h(3)
-        cam_group(5, 0)
-        weave_h(S, 1, 0, 2)
-        fuse(4, 3)
-        weave_h(V, 1, 2, 4)
-        head_passes(0, 0, 0, 3)
-        sigmoid(5, 0)
+        weave_wo(V, 1, 0, 2)
+        cam_group(4, 3)
+        weave_h(S, 3, 0, 2)
         fuse(4, 2)
-        radar_pass(5, 1)
+        cam_group(5, 0)
+        quantise_wo(1)
+        weave_h(S, 3, 2, 4)
+        fuse(4, 3)
+        radar_pass(5, 0)
+        weave_h(V, 2, 2, 4)
         cam_group(5, 1)
-        copy_out(S, 0, 0)
+        sigmoid(5, 0)
+        quantise_h(3)
+        weave_h(S, 4, 0, 2)
+        radar_pass(5, 1)
+        quantise_h(2)
+        radar_pass(5, 2)
+        cam_group(5, 2)
         fuse(5, 0)
         sigmoid(5, 1)
-        quantise_h(1)
-        store(0, 0)
-        head_passes(0, 1, 0, 3)
-        weave_h(S, 4, 0, 2)
-        fuse(5, 1)
-        radar_pass(5, 2)
-        weave_h(V, 4, 2, 4)
-        cam_group(5, 2)
-        copy_out(S, 0, 1)
-        quantise_h(4)
+        cam_group(5, 3)
         sigmoid(5, 2)
-        store(0, 1)
-        head_passes(0, 2, 0, 3)
+        fuse(5, 1)
+        weave_h(S, 4, 2, 4)
         fuse(5, 2)
         radar_pass(5, 3)
-        cam_group(5, 3)
-        copy_out(V, 0, 2)
+        head_passes(0, 0, 0, 3)
         sigmoid(5, 3)
-        store(0, 2)
-        head_passes(0, 3, 0, 3)
+        quantise_h(4)
+        head_passes(0, 1, 0, 3)
+        copy_out(S, 0, 0)
         fuse(5, 3, 0, 128)
+        head_passes(0, 2, 0, 3)
+        weave_h(S, 5, 0, 1)
         fuse(5, 3, 128, 256)
-        head_passes(1, 0, 0, 2)
-        weave_h(V, 5, 0, 1)
+        store(0, 0)
+        copy_out(V, 0, 1)
         weave_h(S, 5, 1, 2)
-        fuse(5, 3, 256, 384)
-        head_passes(1, 1, 0, 2)
+        head_passes(0, 3, 0, 3)
         quantise_h(5, 0, 128)
-        copy_out(S, 0, 3)
-        head_passes(1, 2, 0, 2)
+        store(0, 1)
+        fuse(5, 3, 256, 384)
+        copy_out(S, 0, 2)
         quantise_h(5, 128, 256)
+        head_passes(1, 0, 0, 2)
         weave_h(V, 5, 2, 3)
+        copy_out(S, 0, 3)
         head_passes(1, 0, 2, 3)
+        store(0, 2)
         fuse(5, 3, 384, 512)
+        quantise_h(5, 256, 384)
+        head_passes(1, 1, 0, 2)
+        weave_h(V, 5, 3, 4)
+        copy_out(S, 1, 0)
         store(0, 3)
         head_passes(1, 1, 2, 3)
-        quantise_h(5, 256, 384)
-        weave_h(S, 5, 3, 4)
-        copy_out(V, 1, 0)
-        head_passes(1, 2, 2, 3)
-        copy_out(S, 1, 1)
-        head_passes(1, 3, 0, 2)
+        head_passes(1, 2, 0, 2)
         quantise_h(5, 384, 512)
         store(1, 0)
+        copy_out(S, 1, 1)
+        head_passes(1, 2, 2, 3)
+        head_passes(1, 3, 0, 2)
+        store(1, 1)
         copy_out(V, 1, 2)
         head_passes(1, 3, 2, 3)
-        store(1, 1)
         store(1, 2)
         copy_out(V, 1, 3, 0, 256)
         store(1, 3, 0, 256)

@@ -54,9 +54,13 @@ def tile_camera_radar_gated_fusion_s9_kernel(tc, cam, wc_words, wc_scales, b, ra
         b_rows32 = sb.tile([P, PACK, P], F32, name="b_rows32")
         bias = sb.tile([P, PACK, 4], F32, name="bias")
         chunks = CAM_PASSES + 1
-        cam_raw = tiles("cam_raw", HALVES * 2, [P, TILES, 2 * W], BF16)
+        cam_first = tiles("cam_first", 2, [P, TILES, W], BF16)
+        cam_mid = sb.tile([P, TILES, 2 * W], BF16, name="cam_mid", align_bytes=64)
+        cam_late = sb.tile([P, TILES, KC], BF16, name="cam_late", align_bytes=64)
         radar_raw = tiles("radar_raw", HALVES, [P, TILES, W], BF16)
-        reused = [cam_raw[i // 2][:].rearrange("p i k -> p (i k)")[:, (i % 2) * PACK * W:(i % 2 + 1) * PACK * W] for i in range(8)]
+        reused = [t[:].rearrange("p i k -> p (i k)") for t in cam_first]
+        reused += [cam_mid[:].rearrange("p i k -> p (i k)")[:, i * PACK * W:(i + 1) * PACK * W] for i in range(2)]
+        reused += [cam_late[:, i, :] for i in range(TILES)]
         act_split = tiles("act_split", 6, [P, 2, 2, P], F32)
         act_q = quantised("act", HALVES * chunks)
         act_stage = tiles("act_stage", 3, [P, PACK * W], BF16)
@@ -65,7 +69,9 @@ def tile_camera_radar_gated_fusion_s9_kernel(tc, cam, wc_words, wc_scales, b, ra
         sc_first = sb.tile([P, CAM_PASSES, 128], I32, name="sc_first")
         sc_rest = sb.tile([P, CAM_PASSES, 256], I32, name="sc_rest")
         wc_sc = stack("wc_sc", GROUPS, [P, PACK, CAM_PASSES, P], U8)
-        wr_raw = tiles("wr_raw", GROUPS, [P, PACK, W], BF16)
+        wr_first = sb.tile([P, PACK, W], BF16, name="wr_first")
+        wr_rest = sb.tile([P, PACK, 2 * W], BF16, name="wr_rest")
+        wr_raw = [wr_first[:], wr_rest[:, :, 0:W], wr_rest[:, :, W:2 * W]]
         wo_raw = tiles("wo_raw", GROUPS, [P, PACK, W], BF16)
         w_stage = tiles("w_stage", 2, [P, PACK * W], BF16)
         wr_q = quantised("wr", GROUPS)
@@ -78,13 +84,20 @@ def tile_camera_radar_gated_fusion_s9_kernel(tc, cam, wc_words, wc_scales, b, ra
         h_q = quantised("h", HALVES * GROUPS)
         result = tiles("result", HALVES * TILES, [P, W], F32)
 
-        def load_cam(h, d, lo, hi):
-            rows = cam[h * W:(h + 1) * W, 2 * W * d:2 * W * (d + 1)].rearrange("(p i) k -> p i k", i=TILES)
-            nc.sync.dma_start(out=cam_raw[2 * h + d][:, lo:hi, :], in_=rows[:, lo:hi, :])
+        def load_mid(lo, hi):
+            rows = cam[0:W, 2 * W:4 * W].rearrange("(p i) k -> p i k", i=TILES)
+            nc.sync.dma_start(out=cam_mid[:, lo:hi, :], in_=rows[:, lo:hi, :])
+
+        def load_late(lo, hi):
+            rows = cam[W:2 * W, :].rearrange("(p i) k -> p i k", i=TILES)
+            nc.sync.dma_start(out=cam_late[:, lo:hi, :], in_=rows[:, lo:hi, :])
+
+        def load_wr_rest():
+            nc.sync.dma_start(out=wr_rest[:], in_=wr[:, W:F].rearrange("(p j) c -> p j c", j=PACK))
 
         def load_first(c, lo, hi):
             rows = cam[0:W, c * W:(c + 1) * W].rearrange("(p i) k -> p i k", i=TILES)
-            nc.sync.dma_start(out=h_raw[c][:, lo:hi, :], in_=rows[:, lo:hi, :])
+            nc.sync.dma_start(out=cam_first[c][:, lo:hi, :], in_=rows[:, lo:hi, :])
 
         def load_radar(h):
             nc.sync.dma_start(out=radar_raw[h][:], in_=radar[h * W:(h + 1) * W, :].rearrange("(p i) k -> p i k", i=TILES))
@@ -127,9 +140,14 @@ def tile_camera_radar_gated_fusion_s9_kernel(tc, cam, wc_words, wc_scales, b, ra
                 nc.vector.tensor_copy(out=out, in_=in_)
 
         def halves(h, c):
-            raw = radar_raw[h][:] if c == RADAR else cam_raw[2 * h + c // 2][:, :, (c % 2) * W:(c % 2 + 1) * W]
-            if h == 0 and c < 2:
-                raw = h_raw[c]
+            if c == RADAR:
+                raw = radar_raw[h][:]
+            elif h == 1:
+                raw = cam_late[:, :, c * W:(c + 1) * W]
+            elif c < 2:
+                raw = cam_first[c][:]
+            else:
+                raw = cam_mid[:, :, (c - 2) * W:(c - 1) * W]
             return raw.bitcast(F32).rearrange("p i (w u) -> p i u w", u=2)
 
         def split(engine, h, c, j):
@@ -146,6 +164,10 @@ def tile_camera_radar_gated_fusion_s9_kernel(tc, cam, wc_words, wc_scales, b, ra
                     nc.tensor.transpose(bank[:, col:col + P], words[:, i, u, :], ident[:])
             if is_split:
                 act_split.append(held[("split", h, c, j)])
+
+        def idle_turns(count):
+            for k in range(count):
+                nc.tensor.transpose(banks[-1][:, (k % 4) * P:(k % 4 + 1) * P], ident[:], ident[:])
 
         def unload(engine, h, c, j):
             stage = act_stage[ORDER.index((h, c)) % 3][:].bitcast(F32)
@@ -164,9 +186,10 @@ def tile_camera_radar_gated_fusion_s9_kernel(tc, cam, wc_words, wc_scales, b, ra
             src = wc_raw[G][:, lo:hi, :].rearrange("p g (r t e) -> p t g r e", t=4, e=2)
             nc.vector.tensor_copy(out=dst, in_=src)
 
-        def order_scales(G):
+        def order_scales(G, lo=0, hi=CAM_PASSES):
             raw = sc_first[:] if G == 0 else sc_rest[:, :, 128 * (G - 1):128 * G]
-            nc.vector.tensor_copy(out=wc_sc[G][:].bitcast(I32), in_=raw.rearrange("p g (r t) -> p t g r", t=4))
+            nc.vector.tensor_copy(out=wc_sc[G][:].bitcast(I32)[:, :, lo:hi, :],
+                                  in_=raw.rearrange("p g (r t) -> p t g r", t=4)[:, :, lo:hi, :])
 
         def weave_wr(engine, G, lo, hi):
             dst = w_stage[G % 2][:].rearrange("p (t r e j) -> p t r j e", t=4, e=4, j=4)
@@ -263,268 +286,265 @@ def tile_camera_radar_gated_fusion_s9_kernel(tc, cam, wc_words, wc_scales, b, ra
 
         load_first(0, 0, 2)
         nc.vector.memset(b_rows[:], 0.0)
-        make_identity(nc, ident[:])
-        load_first(0, 2, 4)
-        load_wc(0, 0, 1)
-        load_first(1, 0, 4)
         nc.vector.memset(warm[:, 0:1], 0.0)
         nc.vector.memset(sc_first[:], 0)
-        load_bias()
         nc.vector.memset(sc_rest[:], 0)
-        load_scales(nc.sync, sc_first, 0, 128)
+        load_bias()
         nc.scalar.activation(out=warm[:, 1:2], in_=warm[:, 0:1], func=SIGMOID)
-        load_cam(0, 1, 0, 2)
+        make_identity(nc, ident[:])
+        idle_turns(10)
+        load_first(0, 2, 4)
+        load_scales(nc.sync, sc_first, 0, 128)
+        load_first(1, 0, 4)
+        load_wc(0, 0, 1)
+        load_mid(0, 2)
         turn(0, 0, 0)
-        widen_bias()
-        load_cam(0, 1, 2, 4)
-        turn(0, 0, 1)
-        unload(V, 0, 0, 0)
         load_wc(0, 1, 2)
+        turn(0, 0, 1)
+        widen_bias()
         turn_bias()
-        order_wc(0, 0, 1)
-        unload(S, 0, 0, 1)
-        unload_bias(V)
+        idle_turns(6)
+        unload(S, 0, 0, 0)
+        unload(V, 0, 0, 1)
         quantise_act(0, 0, 0, 256)
-        quantise_act(0, 0, 256, 512)
-        load_wc(0, 2, 4)
-        turn(0, 1, 0)
-        load_wr(0)
+        order_scales(0, 0, 1)
+        unload_bias(S)
+        load_mid(2, 4)
         load_radar(0)
+        load_wr(0)
+        load_wc(0, 2, 4)
+        quantise_act(0, 0, 256, 512)
+        load_wc(1)
+        turn(0, 1, 0)
         load_scales(nc.sync, sc_rest, 128, 384)
+        order_wc(0, 0, 1)
         turn(0, 1, 1)
-        order_scales(0)
         unload(V, 0, 1, 0)
         cam_round(0, 0, 0, 4)
         unload(S, 0, 1, 1)
         split(V, 0, 2, 0)
-        split(S, 0, 3, 0)
         quantise_act(0, 1)
-        split(S, 0, 2, 1)
-        load_wr(1)
+        split(V, 0, 3, 0)
         turn(0, 2, 0)
         order_wc(0, 1, 2)
-        load_wc(1)
+        order_scales(0, 1, 4)
         turn(0, 3, 0)
+        unload(V, 0, 2, 0)
         turn(0, 2, 1)
-        unload(S, 0, 2, 0)
+        unload(S, 0, 3, 0)
+        load_wr_rest()
         turn(0, 3, 1)
-        unload(V, 0, 3, 0)
-        unload(S, 0, 2, 1)
+        unload(V, 0, 2, 1)
         cam_round(0, 1, 0, 4)
-        load_cam(1, 0, 2, 4)
-        weave_wr(V, 0, 2, 4)
-        weave_wr(S, 0, 0, 2)
-        quantise_act(0, 2)
-        load_wr(2)
-        turn(0, 4, 0)
-        split(V, 0, 4, 1)
-        load_cam(1, 1, 0, 2)
         unload(S, 0, 3, 1)
-        order_wc(0, 2, 4)
-        load_cam(1, 0, 0, 2)
-        turn(0, 4, 1)
-        quantise_wr(0)
-        load_radar(1)
-        cam_round(0, 2, 0, 4)
-        unload(S, 0, 4, 0)
+        quantise_act(0, 2)
+        load_late(0, 2)
+        weave_wr(S, 0, 0, 2)
+        turn(0, 4, 0)
+        weave_wr(V, 0, 2, 4)
         load_wc(2)
+        turn(0, 4, 1)
+        order_wc(0, 2, 4)
         quantise_act(0, 3)
+        unload(S, 0, 4, 0)
+        cam_round(0, 2, 0, 4)
+        quantise_wr(0)
         unload(S, 0, 4, 1)
-        order_scales(1)
-        cam_round(0, 3, 0, 2)
-        load_cam(1, 1, 2, 4)
-        weave_wr(S, 1, 0, 2)
+        load_late(2, 4)
+        load_radar(1)
         quantise_act(0, 4)
-        cam_round(0, 3, 2, 4)
-        weave_wr(V, 1, 2, 4)
-        radar_pass(0, 0)
-        radar_pass(0, 1)
+        cam_round(0, 3, 0, 2)
         load_wo(0)
+        cam_round(0, 3, 2, 4)
         order_wc(1)
+        radar_pass(0, 0)
+        order_scales(1)
+        radar_pass(0, 1)
         radar_pass(0, 2)
         sigmoid(0, 0)
-        radar_pass(0, 3)
-        quantise_wr(1)
-        sigmoid(0, 1)
+        order_scales(2)
         cam_group(1, 0)
+        sigmoid(0, 1)
         fuse(0, 0)
         sigmoid(0, 2)
-        fuse(0, 1)
-        split(S, 1, 0, 1)
         cam_group(1, 1)
-        fuse(0, 2)
-        sigmoid(0, 3)
-        weave_wr(V, 2, 2, 4)
-        radar_pass(1, 0)
-        weave_wr(S, 2, 0, 2)
+        fuse(0, 1)
+        weave_wr(S, 1, 2, 4)
+        weave_wr(V, 1, 0, 2)
         cam_group(1, 2)
-        fuse(0, 3)
-        order_scales(2)
-        sigmoid(1, 0)
-        radar_pass(1, 1)
-        radar_pass(1, 2)
-        quantise_wr(2)
-        radar_pass(1, 3)
-        sigmoid(1, 1)
-        load_wo(1)
+        fuse(0, 2)
+        weave_wr(V, 2, 2, 4)
+        weave_wr(S, 2, 0, 2)
+        radar_pass(0, 3)
         cam_group(1, 3)
-        fuse(1, 0)
-        sigmoid(1, 2)
-        fuse(1, 1)
-        split(S, 1, 3, 0)
-        radar_pass(2, 0)
-        turn(1, 0, 0)
-        fuse(1, 2)
-        sigmoid(1, 3)
-        turn(1, 1, 0)
-        split(V, 1, 2, 0)
-        sigmoid(2, 0)
-        unload(V, 1, 0, 0)
-        radar_pass(2, 1)
-        radar_pass(2, 2)
-        unload(S, 1, 1, 0)
-        fuse(1, 3)
-        turn(1, 0, 1)
-        sigmoid(2, 1)
-        turn(1, 1, 1)
-        order_wc(2)
+        quantise_wr(1)
         load_wo(2)
-        turn(1, 2, 0)
+        split(V, 1, 2, 0)
+        sigmoid(0, 3)
+        quantise_wr(2)
+        radar_pass(1, 0)
+        split(S, 1, 3, 0)
+        turn(1, 0, 0)
+        fuse(0, 3)
+        sigmoid(1, 0)
+        order_wc(2)
+        radar_pass(1, 1)
+        unload(S, 1, 0, 0)
+        radar_pass(1, 2)
+        fuse(1, 0)
+        cam_group(2, 0)
+        sigmoid(1, 2)
+        weave_h(V, 0, 0, 2)
+        sigmoid(1, 1)
+        fuse(1, 2)
+        radar_pass(1, 3)
+        turn(1, 1, 0)
+        split(S, 1, 1, 1)
+        fuse(1, 1)
+        turn(1, 0, 1)
+        sigmoid(1, 3)
+        split(V, 1, 3, 1)
+        turn(1, 1, 1)
+        unload(V, 1, 1, 0)
         unload(S, 1, 0, 1)
-        weave_h(V, 0, 2, 4)
+        turn(1, 2, 0)
+        fuse(1, 3)
+        load_wo(1)
         turn(1, 3, 0)
         unload(S, 1, 1, 1)
-        radar_pass(2, 3)
-        unload(V, 1, 2, 0)
-        cam_group(2, 0)
-        sigmoid(2, 2)
-        quantise_act(1, 0)
-        split(S, 1, 3, 1)
-        quantise_act(1, 1)
-        cam_group(2, 1)
-        unload(S, 1, 3, 0)
-        fuse(2, 0)
-        sigmoid(2, 3)
+        split(V, 1, 4, 1)
         turn(1, 2, 1)
-        split(V, 1, 4, 0)
-        fuse(2, 1)
-        split(S, 1, 4, 1)
+        quantise_act(1, 0)
+        unload(S, 1, 2, 0)
         turn(1, 3, 1)
+        quantise_act(1, 1)
         turn(1, 4, 0)
-        weave_wo(V, 1, 2, 4)
         unload(S, 1, 2, 1)
         turn(1, 4, 1)
-        cam_group(2, 2)
+        unload(V, 1, 3, 0)
         unload(S, 1, 3, 1)
-        quantise_act(1, 2)
+        radar_pass(2, 0)
+        unload(S, 1, 4, 0)
+        weave_wo(V, 2, 0, 2)
+        cam_group(2, 1)
         unload(S, 1, 4, 1)
         quantise_act(1, 3)
-        cam_group(2, 3)
-        weave_wo(S, 0, 2, 4)
-        fuse(2, 2)
-        unload(V, 1, 4, 0)
-        cam_group(3, 0)
-        weave_h(S, 1, 0, 2)
-        fuse(2, 3)
+        radar_pass(2, 1)
+        sigmoid(2, 0)
         quantise_act(1, 4)
-        cam_group(3, 1)
-        weave_h(S, 0, 0, 2)
+        radar_pass(2, 2)
+        cam_group(2, 2)
+        sigmoid(2, 2)
+        fuse(2, 0)
+        quantise_act(1, 2)
+        sigmoid(2, 1)
+        radar_pass(2, 3)
+        cam_group(2, 3)
         weave_h(V, 1, 2, 4)
+        sigmoid(2, 3)
+        fuse(2, 1)
+        weave_wo(S, 0, 2, 4)
         radar_pass(3, 0)
-        weave_wo(V, 2, 0, 2)
-        radar_pass(3, 1)
-        cam_group(3, 2)
+        cam_group(3, 0)
+        fuse(2, 3)
+        fuse(2, 2)
         sigmoid(3, 0)
-        quantise_h(0)
-        sigmoid(3, 1)
+        cam_group(3, 1)
+        weave_wo(V, 1, 2, 4)
+        weave_h(S, 0, 2, 4)
         fuse(3, 0)
-        radar_pass(3, 2)
-        weave_h(S, 2, 0, 2)
-        radar_pass(3, 3)
-        fuse(3, 1)
-        cam_group(3, 3)
-        quantise_h(1)
-        sigmoid(3, 2)
+        radar_pass(3, 1)
         weave_wo(V, 2, 2, 4)
-        cam_group(4, 0)
-        sigmoid(3, 3)
-        fuse(3, 2)
-        weave_wo(S, 0, 0, 2)
+        radar_pass(3, 2)
+        radar_pass(3, 3)
+        sigmoid(3, 1)
         radar_pass(4, 0)
-        fuse(3, 3)
-        radar_pass(4, 1)
-        cam_group(4, 1)
+        quantise_h(0)
+        cam_group(3, 2)
+        sigmoid(3, 2)
         quantise_wo(2)
         sigmoid(4, 0)
-        quantise_wo(0)
-        radar_pass(4, 2)
+        fuse(3, 1)
+        radar_pass(4, 1)
+        sigmoid(3, 3)
+        cam_group(3, 3)
+        fuse(3, 2)
         sigmoid(4, 1)
-        radar_pass(4, 3)
+        weave_wo(V, 1, 0, 2)
+        cam_group(4, 0)
+        weave_h(S, 2, 0, 2)
+        fuse(3, 3)
+        quantise_wo(1)
+        cam_group(4, 1)
+        weave_h(S, 2, 2, 4)
         fuse(4, 0)
-        cam_group(4, 2)
+        weave_h(V, 3, 2, 4)
+        radar_pass(4, 2)
+        radar_pass(4, 3)
+        radar_pass(5, 0)
         sigmoid(4, 2)
+        quantise_h(2)
+        cam_group(4, 2)
+        sigmoid(5, 0)
         fuse(4, 1)
         sigmoid(4, 3)
-        weave_wo(V, 1, 0, 2)
+        weave_wo(V, 0, 0, 2)
         cam_group(4, 3)
-        weave_h(S, 3, 0, 2)
+        weave_h(S, 1, 0, 2)
         fuse(4, 2)
         cam_group(5, 0)
-        quantise_wo(1)
-        weave_h(S, 3, 2, 4)
+        quantise_wo(0)
         fuse(4, 3)
-        radar_pass(5, 0)
-        weave_h(V, 2, 2, 4)
-        cam_group(5, 1)
-        sigmoid(5, 0)
-        quantise_h(3)
-        weave_h(S, 4, 0, 2)
+        weave_h(S, 3, 0, 2)
         radar_pass(5, 1)
-        quantise_h(2)
-        radar_pass(5, 2)
-        cam_group(5, 2)
+        cam_group(5, 1)
         fuse(5, 0)
-        sigmoid(5, 1)
-        cam_group(5, 3)
-        sigmoid(5, 2)
-        fuse(5, 1)
+        quantise_h(1)
         weave_h(S, 4, 2, 4)
+        radar_pass(5, 2)
+        weave_h(V, 4, 0, 2)
+        cam_group(5, 2)
+        quantise_h(3)
+        sigmoid(5, 2)
+        quantise_h(4)
+        cam_group(5, 3)
+        sigmoid(5, 1)
         fuse(5, 2)
         radar_pass(5, 3)
+        fuse(5, 1)
         head_passes(0, 0, 0, 3)
         sigmoid(5, 3)
-        quantise_h(4)
         head_passes(0, 1, 0, 3)
-        copy_out(S, 0, 0)
         fuse(5, 3, 0, 128)
-        head_passes(0, 2, 0, 3)
-        weave_h(S, 5, 0, 1)
+        copy_out(S, 0, 0)
         fuse(5, 3, 128, 256)
+        head_passes(0, 2, 0, 3)
+        weave_h(V, 5, 0, 1)
         store(0, 0)
-        copy_out(V, 0, 1)
-        weave_h(S, 5, 1, 2)
+        copy_out(S, 0, 1)
+        fuse(5, 3, 256, 384)
+        weave_h(V, 5, 1, 2)
         head_passes(0, 3, 0, 3)
+        weave_h(S, 5, 2, 3)
         quantise_h(5, 0, 128)
         store(0, 1)
-        fuse(5, 3, 256, 384)
-        copy_out(S, 0, 2)
         quantise_h(5, 128, 256)
-        head_passes(1, 0, 0, 2)
-        weave_h(V, 5, 2, 3)
-        copy_out(S, 0, 3)
-        head_passes(1, 0, 2, 3)
-        store(0, 2)
         fuse(5, 3, 384, 512)
-        quantise_h(5, 256, 384)
-        head_passes(1, 1, 0, 2)
+        copy_out(S, 0, 2)
+        head_passes(1, 0, 0, 2)
         weave_h(V, 5, 3, 4)
+        head_passes(1, 0, 2, 3)
+        copy_out(S, 0, 3)
+        quantise_h(5, 256, 384)
+        store(0, 2)
+        head_passes(1, 1, 0, 2)
+        quantise_h(5, 384, 512)
         copy_out(S, 1, 0)
         store(0, 3)
         head_passes(1, 1, 2, 3)
         head_passes(1, 2, 0, 2)
-        quantise_h(5, 384, 512)
-        store(1, 0)
         copy_out(S, 1, 1)
+        store(1, 0)
         head_passes(1, 2, 2, 3)
         head_passes(1, 3, 0, 2)
         store(1, 1)

from contextlib import ExitStack

import concourse.mybir as mybir
from concourse.masks import make_identity

M, KC, KR, F, N = 1024, 2048, 512, 1536, 512
FLOPS = 2 * M * (KC * F + KR * F + F * N)

F32 = mybir.dt.float32
BF16 = mybir.dt.bfloat16
I32 = mybir.dt.int32
U32 = mybir.dt.uint32
U8 = mybir.dt.uint8
E4M3 = mybir.dt.float8_e4m3fn_x4
E5M2 = mybir.dt.float8_e5m2_x4
E2M1 = mybir.dt.float4_e2m1fn_x4
SIGMOID = mybir.ActivationFunctionType.Sigmoid
ADD = mybir.AluOpType.add
MULT = mybir.AluOpType.mult

P = 128
PACK = 4
W = 512
HALVES = M // W
CAM_PASSES = KC // W
RADAR = CAM_PASSES
GROUPS = F // W
TILES = W // P
ORDER = [(0, 0), (0, 1), (0, 2), (0, 3), (0, RADAR), (1, 0), (1, 1), (1, 2), (1, 3), (1, RADAR)]
UNITS = [(0, 0), (0, 1), (0, 2), (1, 0), (1, 1), (1, 2)]


def tile_camera_radar_gated_fusion_s9_kernel(tc, cam, wc_words, wc_scales, b, radar, wr, wo, out):
    nc = tc.nc
    with ExitStack() as ctx:
        sb = ctx.enter_context(tc.tile_pool(name="sb", bufs=1))
        ps = ctx.enter_context(tc.psum_pool(name="ps", bufs=1))
        ctx.enter_context(tc.manual_schedule())

        def tiles(name, count, shape, dtype):
            return [sb.tile(shape, dtype, name="%s%d" % (name, i), align_bytes=64) for i in range(count)]

        def stack(name, count, shape, dtype):
            whole = sb.tile([P, count] + shape[1:], dtype, name=name, align_bytes=256)
            return [whole[:, i] for i in range(count)]

        def quantised(name, count):
            return list(zip(stack(name + "_codes", count, [P, W], U32), stack(name + "_scales", count, [P, W], U8)))

        banks = [ps.tile([P, W], F32, name="bank%d" % i) for i in range(8)]
        ident = sb.tile([P, P], F32, name="ident")
        warm = sb.tile([P, 8], F32, name="warm")
        b_rows = sb.tile([P, W], BF16, name="b_rows")
        b_rows32 = sb.tile([P, PACK, P], F32, name="b_rows32")
        bias = sb.tile([P, PACK, 4], F32, name="bias")
        chunks = CAM_PASSES + 1
        cam_first = tiles("cam_first", 2, [P, TILES, W], BF16)
        cam_mid = sb.tile([P, TILES, 2 * W], BF16, name="cam_mid", align_bytes=64)
        cam_late = sb.tile([P, TILES, KC], BF16, name="cam_late", align_bytes=64)
        radar_raw = tiles("radar_raw", HALVES, [P, TILES, W], BF16)
        reused = [t[:].rearrange("p i k -> p (i k)") for t in cam_first]
        reused += [cam_mid[:].rearrange("p i k -> p (i k)")[:, i * PACK * W:(i + 1) * PACK * W] for i in range(2)]
        reused += [cam_late[:, i, :] for i in range(TILES)]
        act_split = tiles("act_split", 6, [P, 2, 2, P], F32)
        act_q = quantised("act", HALVES * chunks)
        act_stage = tiles("act_stage", 3, [P, PACK * W], BF16)
        wc_raw = tiles("wc_raw", GROUPS, [P, CAM_PASSES, 256], I32)
        wc_codes = stack("wc_codes", GROUPS, [P, PACK, CAM_PASSES, 256], U8)
        sc_first = sb.tile([P, CAM_PASSES, 128], I32, name="sc_first")
        sc_rest = sb.tile([P, CAM_PASSES, 256], I32, name="sc_rest")
        wc_sc = stack("wc_sc", GROUPS, [P, PACK, CAM_PASSES, P], U8)
        wr_first = sb.tile([P, PACK, W], BF16, name="wr_first")
        wr_rest = sb.tile([P, PACK, 2 * W], BF16, name="wr_rest")
        wr_raw = [wr_first[:], wr_rest[:, :, 0:W], wr_rest[:, :, W:2 * W]]
        wo_raw = tiles("wo_raw", GROUPS, [P, PACK, W], BF16)
        w_stage = tiles("w_stage", 2, [P, PACK * W], BF16)
        wr_q = quantised("wr", GROUPS)
        wo_q = quantised("wo", GROUPS)
        gate = tiles("gate", 6, [P, W], F32)
        h_raw = [reused[n].rearrange("p (t m) -> p t m", t=PACK) for n in range(6)]
        h_own = tiles("h_stage", 2, [P, PACK * W], BF16)
        h_stage = [h_own[0], h_own[1], h_own[0], act_stage[1], act_stage[2], act_stage[0]]
        wo_stage = [radar_raw[0][:].rearrange("p i k -> p (i k)"), reused[6], reused[7]]
        h_q = quantised("h", HALVES * GROUPS)
        result = tiles("result", HALVES * TILES, [P, W], F32)

        def load_mid(lo, hi):
            rows = cam[0:W, 2 * W:4 * W].rearrange("(p i) k -> p i k", i=TILES)
            nc.sync.dma_start(out=cam_mid[:, lo:hi, :], in_=rows[:, lo:hi, :])

        def load_late(lo, hi):
            rows = cam[W:2 * W, :].rearrange("(p i) k -> p i k", i=TILES)
            nc.sync.dma_start(out=cam_late[:, lo:hi, :], in_=rows[:, lo:hi, :])

        def load_wr_rest():
            nc.sync.dma_start(out=wr_rest[:], in_=wr[:, W:F].rearrange("(p j) c -> p j c", j=PACK))

        def load_first(c, lo, hi):
            rows = cam[0:W, c * W:(c + 1) * W].rearrange("(p i) k -> p i k", i=TILES)
            nc.sync.dma_start(out=cam_first[c][:, lo:hi, :], in_=rows[:, lo:hi, :])

        def load_radar(h):
            nc.sync.dma_start(out=radar_raw[h][:], in_=radar[h * W:(h + 1) * W, :].rearrange("(p i) k -> p i k", i=TILES))

        def load_wc(G, lo=0, hi=CAM_PASSES):
            src = wc_words.bitcast(I32)[lo:hi, :, 256 * G:256 * (G + 1)]
            nc.sync.dma_start(out=wc_raw[G][:, lo:hi, :], in_=src.rearrange("g p w -> p g w"))

        def load_scales(queue, dst, lo, hi):
            for Q in range(4):
                src = wc_scales.bitcast(I32)[:, 4 * Q:4 * Q + 4, lo:hi]
                queue.dma_start(out=dst[32 * Q:32 * Q + 4, :, :], in_=src.rearrange("g r w -> r g w"))

        def load_wr(G):
            src = wr[:, G * W:(G + 1) * W].rearrange("(p j) c -> p j c", j=PACK)
            nc.sync.dma_start(out=wr_raw[G][:], in_=src)

        def load_wo(G):
            src = wo[G * W:(G + 1) * W, :].rearrange("(r t e) n -> e r t n", t=4, e=4)
            for e in range(4):
                nc.sync.dma_start(out=wo_raw[G][e:P:4, :, :], in_=src[e])

        def load_bias():
            nc.scalar.dma_start(out=b_rows[0:GROUPS, :], in_=b.rearrange("(G f) -> G f", G=GROUPS))

        S, V = nc.scalar, nc.vector
        held = {}

        def take(key):
            held[key] = banks.pop(0)
            return held[key]

        def give(key):
            banks.append(held[key])

        def copy_on(engine, out, in_):
            if engine is nc.scalar:
                nc.scalar.copy(out=out, in_=in_)
            else:
                nc.vector.tensor_copy(out=out, in_=in_)

        def halves(h, c):
            if c == RADAR:
                raw = radar_raw[h][:]
            elif h == 1:
                raw = cam_late[:, :, c * W:(c + 1) * W]
            elif c < 2:
                raw = cam_first[c][:]
            else:
                raw = cam_mid[:, :, (c - 2) * W:(c - 1) * W]
            return raw.bitcast(F32).rearrange("p i (w u) -> p i u w", u=2)

        def split(engine, h, c, j):
            held[("split", h, c, j)] = act_split.pop(0)
            copy_on(engine, held[("split", h, c, j)][:], halves(h, c)[:, 2 * j:2 * j + 2])

        def turn(h, c, j):
            is_split = ("split", h, c, j) in held
            words = held[("split", h, c, j)][:] if is_split else halves(h, c)[:, 2 * j:2 * j + 2]
            bank = take(("turn", h, c, j))
            for i in range(2):
                for u in range(2):
                    col = (2 * i + u) * P
                    nc.tensor.transpose(bank[:, col:col + P], words[:, i, u, :], ident[:])
            if is_split:
                act_split.append(held[("split", h, c, j)])

        def idle_turns(count):
            for k in range(count):
                nc.tensor.transpose(banks[-1][:, (k % 4) * P:(k % 4 + 1) * P], ident[:], ident[:])

        def unload(engine, h, c, j):
            stage = act_stage[ORDER.index((h, c)) % 3][:].bitcast(F32)
            copy_on(engine, stage[:, j * W:(j + 1) * W].rearrange("p (i r u) -> p i r u", i=2, u=2),
                    held[("turn", h, c, j)][:].rearrange("p (i u r) -> p i r u", i=2, u=2))
            give(("turn", h, c, j))

        def quantise(dst, src, fmt, lo=0, hi=W):
            nc.vector.quantize_mx(out=dst[0][:, lo:hi].bitcast(fmt), scales=dst[1][:, lo:hi], in_=src[:, PACK * lo:PACK * hi])

        def quantise_act(h, c, lo=0, hi=W):
            quantise(act_q[h * chunks + c], act_stage[ORDER.index((h, c)) % 3], E4M3, lo, hi)

        def order_wc(G, lo=0, hi=CAM_PASSES):
            dst = wc_codes[G][:].bitcast(I32)[:, :, lo:hi, :].rearrange("p t g (r e) -> p t g r e", e=2)
            src = wc_raw[G][:, lo:hi, :].rearrange("p g (r t e) -> p t g r e", t=4, e=2)
            nc.vector.tensor_copy(out=dst, in_=src)

        def order_scales(G, lo=0, hi=CAM_PASSES):
            raw = sc_first[:] if G == 0 else sc_rest[:, :, 128 * (G - 1):128 * G]
            nc.vector.tensor_copy(out=wc_sc[G][:].bitcast(I32)[:, :, lo:hi, :],
                                  in_=raw.rearrange("p g (r t) -> p t g r", t=4)[:, :, lo:hi, :])

        def weave_wr(engine, G, lo, hi):
            dst = w_stage[G % 2][:].rearrange("p (t r e j) -> p t r j e", t=4, e=4, j=4)
            src = wr_raw[G][:].rearrange("p j (r t e) -> p t r j e", t=4, e=4)
            if engine is nc.scalar:
                for t in range(lo, hi):
                    nc.scalar.copy(out=dst[:, t], in_=src[:, t])
            else:
                nc.vector.tensor_copy(out=dst[:, lo:hi], in_=src[:, lo:hi])

        def weave(engine, dst, src, lo, hi):
            copy_on(engine, dst[:, lo * W:hi * W].rearrange("p (c i t) -> p c t i", i=4, t=PACK),
                    src[:, :, lo * P:hi * P].rearrange("p t (c i) -> p c t i", i=4))

        def weave_wo(engine, G, lo, hi):
            weave(engine, wo_stage[G], wo_raw[G], lo, hi)

        def weave_h(engine, n, lo, hi):
            weave(engine, h_stage[n], h_raw[n], lo, hi)

        def quantise_h(n, lo=0, hi=W):
            h, G = UNITS[n]
            quantise(h_q[h * GROUPS + G], h_stage[n], E5M2, lo, hi)

        def quantise_wo(G):
            quantise(wo_q[G], wo_stage[G], E4M3)

        def quantise_wr(G):
            quantise(wr_q[G], w_stage[G % 2], E4M3)

        def cam_pass(bank, n, t, g):
            h, G = UNITS[n]
            codes, scales = act_q[h * chunks + g]
            nc.tensor.matmul_mx(out=bank[:], lhsT=wc_codes[G][:, t, g, :].bitcast(E2M1), lhsT_scale=wc_sc[G][:, t, g, :],
                                rhs=codes[:].bitcast(E4M3), rhs_scale=scales[:], start=(g == 0), stop=(g == CAM_PASSES - 1))

        def cam_round(n, g, lo=0, hi=PACK):
            for t in range(lo, hi):
                cam_pass(take(("cam", n, t)) if g == 0 else held[("cam", n, t)], n, t, g)

        def cam_group(n, t):
            bank = take(("cam", n, t))
            for g in range(CAM_PASSES):
                cam_pass(bank, n, t, g)

        def radar_pass(n, t):
            h, G = UNITS[n]
            codes, scales = act_q[h * chunks + RADAR]
            cols = slice(t * P, (t + 1) * P)
            nc.tensor.matmul_mx(out=take(("radar", n, t))[:], lhsT=wr_q[G][0][:, cols].bitcast(E4M3), lhsT_scale=wr_q[G][1][:, cols],
                                rhs=codes[:].bitcast(E4M3), rhs_scale=scales[:], start=True, stop=True)

        def sigmoid(n, t):
            nc.scalar.activation(out=gate[(PACK * n + t) % len(gate)][:], in_=held[("radar", n, t)][:], func=SIGMOID)
            give(("radar", n, t))

        def fuse(n, t, lo=0, hi=W):
            G = UNITS[n][1]
            nc.vector.scalar_tensor_tensor(out=h_raw[n][:, t, lo:hi], in0=held[("cam", n, t)][:, lo:hi], scalar=bias[:, t, G:G + 1],
                                           in1=gate[(PACK * n + t) % len(gate)][:, lo:hi], op0=ADD, op1=MULT)
            if hi == W:
                give(("cam", n, t))

        def head_passes(h, i, lo, hi):
            bank = take(("head", h, i)) if lo == 0 else held[("head", h, i)]
            cols = slice(i * P, (i + 1) * P)
            for G in range(lo, hi):
                codes, scales = h_q[h * GROUPS + G]
                nc.tensor.matmul_mx(out=bank[:], lhsT=codes[:, cols].bitcast(E5M2), lhsT_scale=scales[:, cols],
                                    rhs=wo_q[G][0][:].bitcast(E4M3), rhs_scale=wo_q[G][1][:],
                                    start=(G == 0), stop=(G == GROUPS - 1))

        def copy_out(engine, h, i, lo=0, hi=W):
            copy_on(engine, result[h * TILES + i][:, lo:hi], held[("head", h, i)][:, lo:hi])
            if hi == W:
                give(("head", h, i))

        def store(h, i, lo=0, hi=W):
            rows = out[h * W:(h + 1) * W, lo:hi].rearrange("(p i) n -> p i n", i=TILES)
            nc.sync.dma_start(out=rows[:, i, :], in_=result[h * TILES + i][:, lo:hi])

        def widen_bias():
            nc.vector.tensor_copy(out=b_rows32[:].rearrange("G t (r e) -> G t r e", e=4),
                                  in_=b_rows[:].rearrange("G (r t e) -> G t r e", t=4, e=4))

        def turn_bias():
            bank = take("bias")
            for t in range(PACK):
                nc.tensor.transpose(bank[:, t * P:(t + 1) * P], b_rows32[:, t, :], ident[:])

        def unload_bias(engine):
            copy_on(engine, bias[:], held["bias"][:].rearrange("p (t G) -> p t G", t=PACK)[:, :, 0:4])
            give("bias")

        load_first(0, 0, 2)
        nc.vector.memset(b_rows[:], 0.0)
        nc.vector.memset(warm[:, 0:1], 0.0)
        nc.vector.memset(sc_first[:], 0)
        nc.vector.memset(sc_rest[:], 0)
        load_bias()
        nc.scalar.activation(out=warm[:, 1:2], in_=warm[:, 0:1], func=SIGMOID)
        make_identity(nc, ident[:])
        idle_turns(10)
        load_first(0, 2, 4)
        load_scales(nc.sync, sc_first, 0, 128)
        load_first(1, 0, 4)
        load_wc(0, 0, 1)
        load_mid(0, 2)
        turn(0, 0, 0)
        load_wc(0, 1, 2)
        turn(0, 0, 1)
        widen_bias()
        turn_bias()
        idle_turns(6)
        unload(S, 0, 0, 0)
        unload(V, 0, 0, 1)
        quantise_act(0, 0, 0, 256)
        order_scales(0, 0, 1)
        unload_bias(S)
        load_mid(2, 4)
        load_radar(0)
        load_wr(0)
        load_wc(0, 2, 4)
        quantise_act(0, 0, 256, 512)
        load_wc(1)
        turn(0, 1, 0)
        load_scales(nc.sync, sc_rest, 128, 384)
        order_wc(0, 0, 1)
        turn(0, 1, 1)
        unload(V, 0, 1, 0)
        cam_round(0, 0, 0, 4)
        unload(S, 0, 1, 1)
        split(V, 0, 2, 0)
        quantise_act(0, 1)
        split(V, 0, 3, 0)
        turn(0, 2, 0)
        order_wc(0, 1, 2)
        order_scales(0, 1, 4)
        turn(0, 3, 0)
        unload(V, 0, 2, 0)
        turn(0, 2, 1)
        unload(S, 0, 3, 0)
        load_wr_rest()
        turn(0, 3, 1)
        unload(V, 0, 2, 1)
        cam_round(0, 1, 0, 4)
        unload(S, 0, 3, 1)
        quantise_act(0, 2)
        load_late(0, 2)
        weave_wr(S, 0, 0, 2)
        turn(0, 4, 0)
        weave_wr(V, 0, 2, 4)
        load_wc(2)
        turn(0, 4, 1)
        order_wc(0, 2, 4)
        quantise_act(0, 3)
        unload(S, 0, 4, 0)
        cam_round(0, 2, 0, 4)
        quantise_wr(0)
        unload(S, 0, 4, 1)
        load_late(2, 4)
        load_radar(1)
        quantise_act(0, 4)
        cam_round(0, 3, 0, 2)
        load_wo(0)
        cam_round(0, 3, 2, 4)
        order_wc(1)
        radar_pass(0, 0)
        order_scales(1)
        radar_pass(0, 1)
        radar_pass(0, 2)
        sigmoid(0, 0)
        order_scales(2)
        cam_group(1, 0)
        sigmoid(0, 1)
        fuse(0, 0)
        sigmoid(0, 2)
        cam_group(1, 1)
        fuse(0, 1)
        weave_wr(S, 1, 2, 4)
        weave_wr(V, 1, 0, 2)
        cam_group(1, 2)
        fuse(0, 2)
        weave_wr(V, 2, 2, 4)
        weave_wr(S, 2, 0, 2)
        radar_pass(0, 3)
        cam_group(1, 3)
        quantise_wr(1)
        load_wo(2)
        split(V, 1, 2, 0)
        sigmoid(0, 3)
        quantise_wr(2)
        radar_pass(1, 0)
        split(S, 1, 3, 0)
        turn(1, 0, 0)
        fuse(0, 3)
        sigmoid(1, 0)
        order_wc(2)
        radar_pass(1, 1)
        unload(S, 1, 0, 0)
        radar_pass(1, 2)
        fuse(1, 0)
        cam_group(2, 0)
        sigmoid(1, 2)
        weave_h(V, 0, 0, 2)
        sigmoid(1, 1)
        fuse(1, 2)
        radar_pass(1, 3)
        turn(1, 1, 0)
        split(S, 1, 1, 1)
        fuse(1, 1)
        turn(1, 0, 1)
        sigmoid(1, 3)
        split(V, 1, 3, 1)
        turn(1, 1, 1)
        unload(V, 1, 1, 0)
        unload(S, 1, 0, 1)
        turn(1, 2, 0)
        fuse(1, 3)
        load_wo(1)
        turn(1, 3, 0)
        unload(S, 1, 1, 1)
        split(V, 1, 4, 1)
        turn(1, 2, 1)
        quantise_act(1, 0)
        unload(S, 1, 2, 0)
        turn(1, 3, 1)
        quantise_act(1, 1)
        turn(1, 4, 0)
        unload(S, 1, 2, 1)
        turn(1, 4, 1)
        unload(V, 1, 3, 0)
        unload(S, 1, 3, 1)
        radar_pass(2, 0)
        unload(S, 1, 4, 0)
        weave_wo(V, 2, 0, 2)
        cam_group(2, 1)
        unload(S, 1, 4, 1)
        quantise_act(1, 3)
        radar_pass(2, 1)
        sigmoid(2, 0)
        quantise_act(1, 4)
        radar_pass(2, 2)
        cam_group(2, 2)
        sigmoid(2, 2)
        fuse(2, 0)
        quantise_act(1, 2)
        sigmoid(2, 1)
        radar_pass(2, 3)
        cam_group(2, 3)
        weave_h(V, 1, 2, 4)
        sigmoid(2, 3)
        fuse(2, 1)
        weave_wo(S, 0, 2, 4)
        radar_pass(3, 0)
        cam_group(3, 0)
        fuse(2, 3)
        fuse(2, 2)
        sigmoid(3, 0)
        cam_group(3, 1)
        weave_wo(V, 1, 2, 4)
        weave_h(S, 0, 2, 4)
        fuse(3, 0)
        radar_pass(3, 1)
        weave_wo(V, 2, 2, 4)
        radar_pass(3, 2)
        radar_pass(3, 3)
        sigmoid(3, 1)
        radar_pass(4, 0)
        quantise_h(0)
        cam_group(3, 2)
        sigmoid(3, 2)
        quantise_wo(2)
        sigmoid(4, 0)
        fuse(3, 1)
        radar_pass(4, 1)
        sigmoid(3, 3)
        cam_group(3, 3)
        fuse(3, 2)
        sigmoid(4, 1)
        weave_wo(V, 1, 0, 2)
        cam_group(4, 0)
        weave_h(S, 2, 0, 2)
        fuse(3, 3)
        quantise_wo(1)
        cam_group(4, 1)
        weave_h(S, 2, 2, 4)
        fuse(4, 0)
        weave_h(V, 3, 2, 4)
        radar_pass(4, 2)
        radar_pass(4, 3)
        radar_pass(5, 0)
        sigmoid(4, 2)
        quantise_h(2)
        cam_group(4, 2)
        sigmoid(5, 0)
        fuse(4, 1)
        sigmoid(4, 3)
        weave_wo(V, 0, 0, 2)
        cam_group(4, 3)
        weave_h(S, 1, 0, 2)
        fuse(4, 2)
        cam_group(5, 0)
        quantise_wo(0)
        fuse(4, 3)
        weave_h(S, 3, 0, 2)
        radar_pass(5, 1)
        cam_group(5, 1)
        fuse(5, 0)
        quantise_h(1)
        weave_h(S, 4, 2, 4)
        radar_pass(5, 2)
        weave_h(V, 4, 0, 2)
        cam_group(5, 2)
        quantise_h(3)
        sigmoid(5, 2)
        quantise_h(4)
        cam_group(5, 3)
        sigmoid(5, 1)
        fuse(5, 2)
        radar_pass(5, 3)
        fuse(5, 1)
        head_passes(0, 0, 0, 3)
        sigmoid(5, 3)
        head_passes(0, 1, 0, 3)
        fuse(5, 3, 0, 128)
        copy_out(S, 0, 0)
        fuse(5, 3, 128, 256)
        head_passes(0, 2, 0, 3)
        weave_h(V, 5, 0, 1)
        store(0, 0)
        copy_out(S, 0, 1)
        fuse(5, 3, 256, 384)
        weave_h(V, 5, 1, 2)
        head_passes(0, 3, 0, 3)
        weave_h(S, 5, 2, 3)
        quantise_h(5, 0, 128)
        store(0, 1)
        quantise_h(5, 128, 256)
        fuse(5, 3, 384, 512)
        copy_out(S, 0, 2)
        head_passes(1, 0, 0, 2)
        weave_h(V, 5, 3, 4)
        head_passes(1, 0, 2, 3)
        copy_out(S, 0, 3)
        quantise_h(5, 256, 384)
        store(0, 2)
        head_passes(1, 1, 0, 2)
        quantise_h(5, 384, 512)
        copy_out(S, 1, 0)
        store(0, 3)
        head_passes(1, 1, 2, 3)
        head_passes(1, 2, 0, 2)
        copy_out(S, 1, 1)
        store(1, 0)
        head_passes(1, 2, 2, 3)
        head_passes(1, 3, 0, 2)
        store(1, 1)
        copy_out(V, 1, 2)
        head_passes(1, 3, 2, 3)
        store(1, 2)
        copy_out(V, 1, 3, 0, 256)
        store(1, 3, 0, 256)
        copy_out(V, 1, 3, 256, 512)
        store(1, 3, 256, 512)
